import numpy as np
import ml_dtypes


def mxq(x, axis, fmt="e4m3"):
    dtype, down = {"e4m3": (ml_dtypes.float8_e4m3fn, 7), "e5m2": (ml_dtypes.float8_e5m2, 14)}[fmt]
    v = np.moveaxis(np.asarray(x, np.float32).astype(ml_dtypes.bfloat16).astype(np.float64), axis, -1)
    blocks = v.reshape(v.shape[:-1] + (-1, 32))
    amax = np.abs(blocks).max(-1, keepdims=True)
    byte = np.maximum(np.where(amax > 0, np.frexp(amax)[1] - 1 + 127, 0) - down, 1)
    scale = np.exp2(byte - 127.0)
    codes = (blocks / scale).astype(np.float32).astype(dtype).astype(np.float64)
    return np.moveaxis((codes * scale).reshape(v.shape), -1, axis)


WIDE = False


def mx_kscale(k):
    if not WIDE:
        return np.ones(k)
    levels = np.array([10, -10, 5, -5, 0])
    if k % 512:
        return np.exp2(np.random.permutation(np.resize(levels, k // 32))).repeat(32)
    a = np.empty((k // 512, 16))
    for p in range(k // 512):
        a[p, :8] = np.random.permutation(np.resize(levels, 8))
        for g in range(8):
            far = levels[np.abs(levels - a[p, g]) >= 10]
            a[p, g + 8] = far[np.random.randint(len(far))]
    return np.exp2(a.ravel()).repeat(32)


BF16 = ml_dtypes.bfloat16


def bf(x):
    return np.asarray(x, np.float32).astype(BF16)


def f64(x):
    return np.asarray(x).astype(np.float64)


E2M1 = np.array([0.0, 0.5, 1.0, 1.5, 2.0, 3.0, 4.0, 6.0, -0.0, -0.5, -1.0, -1.5, -2.0, -3.0, -4.0, -6.0])


def pack_weight(w, fmt):
    k, n = w.shape
    w = f64(bf(w)).reshape(k // 32, 32, n)
    amax = np.abs(w).max(1)
    if fmt == "e4m3":
        byte = np.frexp(amax)[1] - 1 + 127 - 7
    else:
        mant, ex = np.frexp(amax / 6.0)
        byte = np.where(mant > 0.5, ex, ex - 1) + 127
    byte = np.clip(np.where(amax > 0, byte, 1), 1, 254)
    scaled = (w * np.exp2(127.0 - byte)[:, None, :]).reshape(k, n).astype(np.float32)
    by_word = np.ascontiguousarray(scaled.reshape(k // 512, 128, 4, n).transpose(0, 1, 3, 2))
    if fmt == "e4m3":
        words = by_word.astype(ml_dtypes.float8_e4m3fn).view(np.uint8)
    else:
        c = by_word.astype(ml_dtypes.float4_e2m1fn).view(np.uint8) & 0xF
        words = c[..., 0::2] | (c[..., 1::2] << 4)
    return np.ascontiguousarray(words), np.ascontiguousarray(byte.astype(np.uint8).reshape(k // 512, 16, n))


def unpack_weight(words, scales, fmt):
    g, p, n, _ = words.shape
    if fmt == "e4m3":
        vals = np.ascontiguousarray(words).view(ml_dtypes.float8_e4m3fn).astype(np.float64)
    else:
        nib = np.empty((g, p, n, 4), np.uint8)
        nib[..., 0::2] = words & 0xF
        nib[..., 1::2] = words >> 4
        vals = E2M1[nib]
    vals = vals * np.repeat(np.exp2(scales.astype(np.float64) - 127.0), 8, axis=1)[..., None]
    return vals.transpose(0, 1, 3, 2).reshape(g * 512, n)

def planes(Y):
    n, m = Y.shape
    b = f64(bf(Y)).reshape(n // 32, 32, m)
    amax = np.abs(b).max(1)
    byte = np.clip(np.where(amax > 0, np.frexp(amax)[1] - 1 + 127 - 7, 1), 1, 254)
    codes = (b * np.exp2(127.0 - byte)[:, None, :]).reshape(n, m).astype(np.float32).astype(ml_dtypes.float8_e4m3fn).view(np.uint8)
    words = codes.reshape(n // 512, 128, 4, m).transpose(0, 1, 3, 2)
    return np.ascontiguousarray(words), np.ascontiguousarray(byte.astype(np.uint8).reshape(n // 512, 16, m))


B, S, D = 2, 512, 512
TWO = 2


def softmax_last(logit):
    top = np.max(logit, axis=-1, keepdims=True)
    e = np.exp(logit - top)
    return e / np.sum(e, axis=-1, keepdims=True)


def setup_inputs():
    s, t = mx_kscale(D), mx_kscale(S)
    x = bf(np.random.standard_normal((B, S, D)) * s)
    w_words, w_scales = pack_weight(np.random.standard_normal((D, S)) * (2.0 / np.sqrt(D)) / s[:, None], "e4m3")
    rnd = bf(np.random.standard_normal((S, S)) * 1.5)
    mix = bf(np.random.uniform(0.5, 0.9, (TWO,)))
    wv_words, wv_scales = pack_weight(np.random.standard_normal((D, D)) / np.sqrt(D) / s[:, None], "e4m3")
    c = bf(np.random.standard_normal(S) * (0.25 * np.sqrt(S)) * t)
    u = bf((1.0 + 0.1 * np.random.standard_normal(S)) / t)
    return {"x": x, "w_words": w_words, "w_scales": w_scales, "rnd": rnd, "mix": mix, "wv_words": wv_words, "wv_scales": wv_scales, "c": c, "u": u}


def core(x, w_words, w_scales, rnd, mix, wv_words, wv_scales, c, u):
    mix = f64(mix)
    xq = mxq(f64(x), 2, "e4m3")
    syn = xq @ unpack_weight(w_words, w_scales, "e4m3")
    logit = mix[0] * syn + mix[1] * f64(rnd)[None, :, :]
    p = softmax_last(logit)
    pc = p * f64(c)[None, None, :]
    v = f64(u)[None, :, None] * (xq @ unpack_weight(wv_words, wv_scales, "e4m3"))
    return mxq(pc, 2, "e4m3") @ mxq(v, 1, "e4m3")


def reference(x, w_words, w_scales, rnd, mix, wv_words, wv_scales, c, u):
    R_out = core(x, w_words, w_scales, rnd, mix, wv_words, wv_scales, c, u)
    words, scales = planes(np.moveaxis(R_out, 2, 0).reshape(512, -1))
    return R_out, words, scales

@@ -1,0 +1,432 @@
+from contextlib import ExitStack
+
+import concourse.mybir as mybir
+from concourse.masks import make_identity
+
+B, S, D = 2, 512, 512
+FLOPS = 3 * 2 * B * S * S * D
+
+F32 = mybir.dt.float32
+BF16 = mybir.dt.bfloat16
+U32 = mybir.dt.uint32
+I32 = mybir.dt.int32
+U8 = mybir.dt.uint8
+X4 = mybir.dt.float8_e4m3fn_x4
+ALU = mybir.AluOpType
+ACT = mybir.ActivationFunctionType
+AXIS = mybir.AxisListType
+
+P = 128
+PACK = 4
+TILES = S // P
+N_TILES = B * TILES
+MANUAL_ORDER = True
+
+
+def tile_mixturedenserandomsynthesizer_x2_kernel(
+    tc, x, w_words, w_scales, rnd, mix, wv_words, wv_scales, c, u, out_0, out_1, out_2
+):
+    nc = tc.nc
+    with ExitStack() as ctx:
+        keep = ctx.enter_context(tc.tile_pool(name="keep", bufs=1))
+        work = ctx.enter_context(tc.tile_pool(name="work", bufs=4))
+        psum = ctx.enter_context(tc.psum_pool(name="psum", bufs=2))
+
+        x_sb = [keep.tile([P, TILES, D], BF16, name="x_sb%d" % b) for b in range(B)]
+        w_sb = keep.tile([P, S], U32, name="w_sb", align_bytes=64)
+        wv_sb = keep.tile([P, D], U32, name="wv_sb", align_bytes=64)
+        ws_sb = keep.tile([P, S], U8, name="ws_sb", align_bytes=64)
+        wvs_sb = keep.tile([P, D], U8, name="wvs_sb", align_bytes=64)
+        rnd_sb = keep.tile([P, TILES, S], BF16, name="rnd_sb")
+        rm = keep.tile([P, TILES, S], F32, name="rm")
+        mix_bf = keep.tile([P, 2], BF16, name="mix_bf")
+        mix_f = keep.tile([P, 2], F32, name="mix_f")
+        u_bf = keep.tile([P, TILES], BF16, name="u_bf")
+        c_row = keep.tile([P, S], BF16, name="c_row")
+        u_f = keep.tile([P, TILES], F32, name="u_f")
+        vn = keep.tile([P, PACK, D], BF16, name="vn", align_bytes=64)
+        ones = keep.tile([P, P], BF16, name="ones")
+        ident = keep.tile([P, P], F32, name="ident")
+        warm = keep.tile([P, 1], F32, name="warm")
+
+        x_v = [x[b].rearrange("(p t) f -> p t f", t=TILES) for b in range(B)]
+        rnd_v = rnd.rearrange("(p t) k -> p t k", t=TILES)
+
+        nc.vector.memset(ws_sb[:].bitcast(I32), 0)
+        nc.vector.memset(wvs_sb[:].bitcast(I32), 0)
+        nc.vector.memset(warm[:], 0.0)
+        nc.vector.memset(c_row[:], 0.0)
+        nc.vector.memset(ones[:], 1.0)
+        make_identity(nc, ident[:])
+
+        def load_scales(dst, src):
+            for q in range(4):
+                nc.sync.dma_start(
+                    out=dst[32 * q : 32 * q + 4, :].bitcast(I32),
+                    in_=src[0, 4 * q : 4 * q + 4, :].bitcast(I32),
+                )
+
+        def load_words(dst, src):
+            nc.sync.dma_start(
+                out=dst[:].bitcast(I32), in_=src[0].rearrange("p n t -> p (n t)").bitcast(I32)
+            )
+
+        nc.scalar.dma_start(out=mix_bf[:], in_=mix.partition_broadcast(P))
+        nc.scalar.activation(out=warm[:], in_=warm[:], func=ACT.Exp)
+        nc.sync.dma_start(out=x_sb[0][:, 0:2, :], in_=x_v[0][:, 0:2, :])
+        load_scales(ws_sb, w_scales)
+        nc.sync.dma_start(out=rnd_sb[:, 0:1, :], in_=rnd_v[:, 0:1, :])
+        load_words(w_sb, w_words)
+        nc.sync.dma_start(out=x_sb[0][:, 2:4, :], in_=x_v[0][:, 2:4, :])
+        nc.gpsimd.dma_start(out=rnd_sb[:, 1:2, :], in_=rnd_v[:, 1:2, :])
+        nc.gpsimd.dma_start(out=u_bf[:], in_=u.rearrange("(p t) -> p t", t=TILES))
+        nc.gpsimd.dma_start(out=c_row[0:1, :], in_=c.rearrange("(o k) -> o k", o=1))
+        load_scales(wvs_sb, wv_scales)
+        load_words(wv_sb, wv_words)
+        nc.sync.dma_start(out=rnd_sb[:, 2:4, :], in_=rnd_v[:, 2:4, :])
+        nc.sync.dma_start(out=x_sb[1][:], in_=x_v[1])
+
+        c_ps = psum.tile([P, S], F32, name="c_ps", bufs=1)
+
+        def rnd_mix(t, eng):
+            if eng == "v":
+                nc.vector.tensor_scalar(
+                    out=rm[:, t, :], in0=rnd_sb[:, t, :], scalar1=mix_f[:, 1:2], scalar2=None, op0=ALU.mult
+                )
+            else:
+                nc.scalar.activation(
+                    out=rm[:, t, :], in_=rnd_sb[:, t, :], func=ACT.Copy, scale=mix_f[:, 1:2]
+                )
+
+        xq = [keep.tile([P, S], U32, name="xq%d" % b, align_bytes=64) for b in range(B)]
+        xs = [keep.tile([P, S], U8, name="xs%d" % b, align_bytes=64) for b in range(B)]
+        vg = [keep.tile([P, D, PACK], BF16, name="vg%d" % b, align_bytes=64) for b in range(B)]
+        vq = [keep.tile([P, D], U32, name="vq%d" % b, align_bytes=64) for b in range(B)]
+        vs = [keep.tile([P, D], U8, name="vs%d" % b, align_bytes=64) for b in range(B)]
+        og = [keep.tile([P, S, PACK], BF16, name="og%d" % b, align_bytes=64) for b in range(B)]
+        oq = [keep.tile([P, S], U32, name="oq%d" % b, align_bytes=64) for b in range(B)]
+        os_ = [keep.tile([P, S], U8, name="os%d" % b, align_bytes=64) for b in range(B)]
+
+        state = {}
+
+        def x_turn(n):
+            b, t = divmod(n, TILES)
+            words = x_sb[b][:, t, :].bitcast(F32)
+            xt = psum.tile([P, 2, P], F32, name="turn")
+            for h in range(2):
+                nc.tensor.transpose(xt[:, h, :], words[:, h : 2 * P : 2], ident[:])
+            xg = work.tile([P, P, PACK], BF16, name="xg", align_bytes=64)
+            nc.scalar.copy(
+                out=xg[:].rearrange("p n j -> p (n j)").bitcast(F32).rearrange("p (n h) -> p n h", h=2),
+                in_=xt[:].rearrange("p h n -> p n h"),
+            )
+            state["xg", n] = xg
+
+        def x_quant(n):
+            b, t = divmod(n, TILES)
+            cols = slice(P * t, P * (t + 1))
+            nc.vector.quantize_mx(
+                out=xq[b][:, cols].bitcast(X4), scales=xs[b][:, cols],
+                in_=state["xg", n][:].rearrange("p n j -> p (n j)"),
+            )
+
+        def syn(n):
+            b, t = divmod(n, TILES)
+            cols = slice(P * t, P * (t + 1))
+            ps = psum.tile([P, S], F32, name="syn_ps")
+            nc.tensor.matmul_mx(
+                out=ps[:], lhsT=xq[b][:, cols].bitcast(X4), lhsT_scale=xs[b][:, cols],
+                rhs=w_sb[:].bitcast(X4), rhs_scale=ws_sb[:], start=True, stop=True,
+            )
+            state["syn", n] = ps
+
+        def logit(n):
+            t = n % TILES
+            lg = work.tile([P, S], F32, name="lg")
+            nc.vector.scalar_tensor_tensor(
+                out=lg[:], in0=state["syn", n][:], scalar=mix_f[:, 0:1], in1=rm[:, t, :],
+                op0=ALU.mult, op1=ALU.add,
+            )
+            state["lg", n] = lg
+
+        def row_max(n):
+            nmax = work.tile([P, 1], F32, name="nmax")
+            nc.vector.tensor_reduce(
+                out=nmax[:], in_=state["lg", n][:], axis=AXIS.X, op=ALU.max, negate=True
+            )
+            state["nmax", n] = nmax
+
+        def expo(n):
+            e = work.tile([P, S], F32, name="e")
+            tot = work.tile([P, 1], F32, name="tot")
+            nc.scalar.activation(
+                out=e[:], in_=state["lg", n][:], func=ACT.Exp, bias=state["nmax", n][:],
+                scale=1.0, accum_out=tot[:],
+            )
+            state["e", n], state["tot", n] = e, tot
+
+        def recip(n):
+            rinv = work.tile([P, 1], F32, name="rinv")
+            nc.vector.reciprocal(rinv[:], state["tot", n][:])
+            state["rinv", n] = rinv
+
+        def pc(n):
+            pcs = work.tile([P, S], BF16, name="pcs", align_bytes=64)
+            nc.vector.scalar_tensor_tensor(
+                out=pcs[:], in0=state["e", n][:], scalar=state["rinv", n][:], in1=c_ps[:],
+                op0=ALU.mult, op1=ALU.mult,
+            )
+            state["pcs", n] = pcs
+
+        def p_turn(n):
+            words = state["pcs", n][:].bitcast(F32)
+            pt = psum.tile([P, 2, P], F32, name="turn")
+            for h in range(2):
+                nc.tensor.transpose(pt[:, h, :], words[:, h : 2 * P : 2], ident[:])
+            state["pt", n] = pt
+
+        def p_evac(n):
+            pg = work.tile([P, P, PACK], BF16, name="pg", align_bytes=64)
+            nc.scalar.copy(
+                out=pg[:].rearrange("p n j -> p (n j)").bitcast(F32).rearrange("p (n h) -> p n h", h=2),
+                in_=state["pt", n][:].rearrange("p h n -> p n h"),
+            )
+            state["pg", n] = pg
+
+        def p_quant(n):
+            pq = work.tile([P, P], U32, name="pq", align_bytes=64)
+            pqs = work.tile([P, P], U8, name="pqs", align_bytes=64)
+            nc.vector.quantize_mx(
+                out=pq[:].bitcast(X4), scales=pqs[:],
+                in_=state["pg", n][:].rearrange("p n j -> p (n j)"),
+            )
+            state["pq", n] = (pq, pqs)
+
+        def v_mm(i):
+            b, ch = divmod(i, TILES)
+            ps = psum.tile([P, PACK, P], F32, name="quad_ps")
+            dcols = slice(P * ch, P * (ch + 1))
+            for t in range(PACK):
+                cols = slice(P * t, P * (t + 1))
+                nc.tensor.matmul_mx(
+                    out=ps[:, t, :], lhsT=xq[b][:, cols].bitcast(X4), lhsT_scale=xs[b][:, cols],
+                    rhs=wv_sb[:, dcols].bitcast(X4), rhs_scale=wvs_sb[:, dcols], start=True, stop=True,
+                )
+            state["vps", i] = ps
+
+        def v_gain(i):
+            b, ch = divmod(i, TILES)
+            m = P // PACK
+            nc.vector.tensor_tensor(
+                out=vg[b][:].rearrange("p (d m) t -> p d m t", d=PACK)[:, :, m * ch : m * (ch + 1), :],
+                in0=state["vps", i][:].rearrange("p t (m d) -> p d m t", d=PACK),
+                in1=u_bf[:].unsqueeze(1).unsqueeze(1).to_broadcast([P, PACK, m, PACK]),
+                op=ALU.mult,
+            )
+
+        def v0_slot(t):
+            cols = slice(P * t, P * (t + 1))
+            ps = psum.tile([P, D], F32, name="quad_ps")
+            nc.tensor.matmul_mx(
+                out=ps[:], lhsT=xq[0][:, cols].bitcast(X4), lhsT_scale=xs[0][:, cols],
+                rhs=wv_sb[:].bitcast(X4), rhs_scale=wvs_sb[:], start=True, stop=True,
+            )
+            nc.scalar.activation(
+                out=vn[:, t, :].rearrange("p (d m) -> p d m", d=PACK),
+                in_=ps[:].rearrange("p (m d) -> p d m", d=PACK),
+                func=ACT.Copy, scale=u_f[:, t : t + 1],
+            )
+
+        def v0_pack():
+            nc.vector.tensor_copy(
+                out=vg[0][:].rearrange("p (c i) t -> p c t i", i=PACK),
+                in_=vn[:].rearrange("p t (c i) -> p c t i", i=PACK),
+            )
+
+        def v_quant(b):
+            nc.vector.quantize_mx(
+                out=vq[b][:].bitcast(X4), scales=vs[b][:], in_=vg[b][:].rearrange("p n j -> p (n j)")
+            )
+
+        def nat_mm(nat, n):
+            b = n // TILES
+            pq, pqs = state["pq", n]
+            nc.tensor.matmul_mx(
+                out=nat[:], lhsT=pq[:].bitcast(X4), lhsT_scale=pqs[:],
+                rhs=vq[b][:].bitcast(X4), rhs_scale=vs[b][:], start=True, stop=True,
+            )
+
+        def out_mm(n):
+            b = n // TILES
+            pq, pqs = state["pq", n]
+            qd = psum.tile([P, PACK, P], F32, name="quad_ps")
+            if n == N_TILES - 1:
+                nat = psum.tile([P, D], F32, name="syn_ps")
+                nat_mm(nat, n)
+            for d in range(PACK):
+                cols = slice(P * d, P * (d + 1))
+                nc.tensor.matmul_mx(
+                    out=qd[:, d, :], lhsT=vq[b][:, cols].bitcast(X4), lhsT_scale=vs[b][:, cols],
+                    rhs=pq[:].bitcast(X4), rhs_scale=pqs[:], start=True, stop=True,
+                )
+            if n < N_TILES - 1:
+                if n == N_TILES - 3:
+                    nat = psum.tile([P, D], F32, name="syn_ps")
+                else:
+                    nat = psum.tile([P, D], F32, name="nat_ps", bufs=1)
+                nat_mm(nat, n)
+            state["qd", n], state["nat", n] = qd, nat
+
+        def nat_evac(n, eng):
+            ob = work.tile([P, D], F32, name="ob")
+            state["ob", n] = ob
+            src = state["nat", n][:].rearrange("p (d m) -> p m d", d=PACK)
+            dst = ob[:].rearrange("p (m d) -> p m d", d=PACK)
+            if eng == "s":
+                nc.scalar.copy(out=dst, in_=src)
+            else:
+                nc.vector.tensor_copy(out=dst, in_=src)
+
+        def nat_store(n, eng):
+            b, t = divmod(n, TILES)
+            eng.dma_start(out=out_0[b].rearrange("(p t) d -> p t d", t=TILES)[:, t, :], in_=state["ob", n][:])
+
+        def quad_evac(n, p0, p1, eng):
+            b, t = divmod(n, TILES)
+            (nc.scalar.copy if eng == "s" else nc.vector.tensor_copy)(
+                out=og[b][:].rearrange("m (p t) d -> m t p d", t=TILES)[:, t, p0:p1, :],
+                in_=state["qd", n][:].rearrange("m d p -> m p d")[:, p0:p1, :],
+            )
+
+        def o_quant(b, i0, i1):
+            nc.vector.quantize_mx(
+                out=oq[b][:, i0:i1].bitcast(X4), scales=os_[b][:, i0:i1],
+                in_=og[b][:, i0:i1, :].rearrange("m i d -> m (i d)"),
+            )
+
+        def o_store(b, i0, i1):
+            nc.sync.dma_start(
+                out=out_1[0][:, S * b + i0 : S * b + i1, :].rearrange("m i d -> m (i d)").bitcast(I32),
+                in_=oq[b][:, i0:i1].bitcast(I32),
+            )
+
+        def o_scales(b):
+            for q in range(4):
+                nc.sync.dma_start(
+                    out=out_2[0, 4 * q : 4 * q + 4, S * b : S * (b + 1)].bitcast(I32),
+                    in_=os_[b][32 * q : 32 * q + 4, :].bitcast(I32),
+                )
+
+        V_CHUNKS = {4: [4], 5: [5], 6: [6, 7]}
+        X_AHEAD = {3: [4, 5, 6, 7]}
+        LAST = N_TILES - 1
+
+        def live(n):
+            return 0 <= n < N_TILES
+
+        def body():
+            x_turn(0)
+            x_turn(1)
+            nc.vector.tensor_copy(out=mix_f[:], in_=mix_bf[:])
+            rnd_mix(1, "s")
+            x_quant(0)
+            syn(0)
+            rnd_mix(0, "v")
+            x_quant(1)
+            syn(1)
+            logit(0)
+            x_turn(2)
+            x_turn(3)
+            row_max(0)
+            expo(0)
+            x_quant(2)
+            x_quant(3)
+            nc.vector.tensor_copy(out=u_f[:], in_=u_bf[:])
+            v0_slot(0)
+            v0_slot(1)
+            nc.tensor.matmul(c_ps[:], lhsT=ones[:], rhs=c_row[:], start=True, stop=True)
+            for k in range(1, N_TILES):
+                if live(k - 2):
+                    p_turn(k - 2)
+                if live(k - 3):
+                    out_mm(k - 3)
+                logit(k)
+                recip(k - 1)
+                if live(k - 2):
+                    p_evac(k - 2)
+                if live(k - 3):
+                    quad_evac(k - 3, 0, P, "s")
+                for n in X_AHEAD.get(k, []):
+                    x_quant(n)
+                for i in V_CHUNKS.get(k, [])[:1]:
+                    v_gain(i)
+                if k == 1:
+                    rnd_mix(2, "v")
+                if k == 2:
+                    rnd_mix(3, "v")
+                if k == LAST:
+                    p_quant(k - 2)
+                    pc(k - 1)
+                row_max(k)
+                expo(k)
+                if k == 2:
+                    v0_pack()
+                for i in V_CHUNKS.get(k, [])[1:]:
+                    v_mm(i)
+                    v_gain(i)
+                if k == LAST:
+                    break
+                if live(k - 3):
+                    nat_evac(k - 3, "s")
+                    nat_store(k - 3, nc.sync)
+                if live(k - 2):
+                    p_quant(k - 2)
+                if k == 2:
+                    v_quant(0)
+                pc(k - 1)
+                if k == LAST - 1:
+                    v_quant(1)
+                if live(k + 1):
+                    syn(k + 1)
+                if k == 1:
+                    v0_slot(2)
+                    v0_slot(3)
+                for n in X_AHEAD.get(k + 1, []):
+                    x_turn(n)
+                for i in V_CHUNKS.get(k + 1, [])[:1]:
+                    v_mm(i)
+            p_turn(LAST - 1)
+            out_mm(LAST - 2)
+            o_quant(0, 0, S)
+            o_store(0, 0, S)
+            o_scales(0)
+            recip(LAST)
+            p_evac(LAST - 1)
+            pc(LAST)
+            nat_evac(LAST - 3, "s")
+            nat_store(LAST - 3, nc.sync)
+            nat_evac(LAST - 2, "s")
+            nat_store(LAST - 2, nc.sync)
+            p_turn(LAST)
+            p_quant(LAST - 1)
+            out_mm(LAST - 1)
+            p_evac(LAST)
+            quad_evac(LAST - 2, 0, P, "v")
+            p_quant(LAST)
+            quad_evac(LAST - 1, 0, P, "s")
+            out_mm(LAST)
+            nat_evac(LAST - 1, "v")
+            nat_store(LAST - 1, nc.sync)
+            nat_evac(LAST, "v")
+            nat_store(LAST, nc.sync)
+            quad_evac(LAST, 0, P // 2, "s")
+            quad_evac(LAST, P // 2, P, "s")
+            o_quant(1, 0, S // 2)
+            o_store(1, 0, S // 2)
+            o_quant(1, S // 2, S)
+            o_store(1, S // 2, S)
+            o_scales(1)
+
+        if MANUAL_ORDER:
+            ctx.enter_context(tc.manual_schedule())
+        body()

@@ -20,7 +20,7 @@ P = 128
 PACK = 4
 TILES = S // P
 N_TILES = B * TILES
-MANUAL_ORDER = True
+PAIR = 2
 
 
 def tile_mixturedenserandomsynthesizer_x2_kernel(
@@ -31,33 +31,65 @@ def tile_mixturedenserandomsynthesizer_x2_kernel(
         keep = ctx.enter_context(tc.tile_pool(name="keep", bufs=1))
         work = ctx.enter_context(tc.tile_pool(name="work", bufs=4))
         psum = ctx.enter_context(tc.psum_pool(name="psum", bufs=2))
+        ctx.enter_context(tc.manual_schedule())
 
-        x_sb = [keep.tile([P, TILES, D], BF16, name="x_sb%d" % b) for b in range(B)]
+        x_groups = [(0, 1), (1, 2), (2, 4), (4, 8)]
+        rnd_groups = [(0, 1), (1, 2), (2, 4)]
+        x_sb = [keep.tile([P, n1 - n0, D], BF16, name="x_sb%d" % n0) for n0, n1 in x_groups]
+        rnd_sb = [keep.tile([P, t1 - t0, S], BF16, name="rnd_sb%d" % t0) for t0, t1 in rnd_groups]
         w_sb = keep.tile([P, S], U32, name="w_sb", align_bytes=64)
         wv_sb = keep.tile([P, D], U32, name="wv_sb", align_bytes=64)
         ws_sb = keep.tile([P, S], U8, name="ws_sb", align_bytes=64)
         wvs_sb = keep.tile([P, D], U8, name="wvs_sb", align_bytes=64)
-        rnd_sb = keep.tile([P, TILES, S], BF16, name="rnd_sb")
         rm = keep.tile([P, TILES, S], F32, name="rm")
         mix_bf = keep.tile([P, 2], BF16, name="mix_bf")
         mix_f = keep.tile([P, 2], F32, name="mix_f")
-        u_bf = keep.tile([P, TILES], BF16, name="u_bf")
-        c_row = keep.tile([P, S], BF16, name="c_row")
+        u_bf = keep.tile([P, 8], BF16, name="u_bf")
         u_f = keep.tile([P, TILES], F32, name="u_f")
-        vn = keep.tile([P, PACK, D], BF16, name="vn", align_bytes=64)
+        c_row = keep.tile([P, S], BF16, name="c_row")
         ones = keep.tile([P, P], BF16, name="ones")
         ident = keep.tile([P, P], F32, name="ident")
-        warm = keep.tile([P, 1], F32, name="warm")
+        c_ps = psum.tile([P, S], F32, name="c_ps", bufs=1)
 
-        x_v = [x[b].rearrange("(p t) f -> p t f", t=TILES) for b in range(B)]
-        rnd_v = rnd.rearrange("(p t) k -> p t k", t=TILES)
+        xq = [keep.tile([P, S], U32, name="xq%d" % b, align_bytes=64) for b in range(B)]
+        xs = [keep.tile([P, S], U8, name="xs%d" % b, align_bytes=64) for b in range(B)]
+        vn = [keep.tile([P, PACK, D], BF16, name="vn%d" % b, align_bytes=64) for b in range(B)]
+        vg = [keep.tile([P, D, PACK], BF16, name="vg%d" % b, align_bytes=64) for b in range(B)]
+        vq = [keep.tile([P, D], U32, name="vq%d" % b, align_bytes=64) for b in range(B)]
+        vs = [keep.tile([P, D], U8, name="vs%d" % b, align_bytes=64) for b in range(B)]
+        og = [keep.tile([P, S, PACK], BF16, name="og%d" % b, align_bytes=64) for b in range(B)]
+        oq = [keep.tile([P, S], U32, name="oq%d" % b, align_bytes=64) for b in range(B)]
+        os_ = [keep.tile([P, S], U8, name="os%d" % b, align_bytes=64) for b in range(B)]
+        pq = [keep.tile([P, P], U32, name="pq%d" % n, align_bytes=64) for n in range(N_TILES)]
+        pqs = [keep.tile([P, P], U8, name="pqs%d" % n, align_bytes=64) for n in range(N_TILES)]
 
-        nc.vector.memset(ws_sb[:].bitcast(I32), 0)
-        nc.vector.memset(wvs_sb[:].bitcast(I32), 0)
-        nc.vector.memset(warm[:], 0.0)
-        nc.vector.memset(c_row[:], 0.0)
-        nc.vector.memset(ones[:], 1.0)
-        make_identity(nc, ident[:])
+        state = {}
+
+        def spread_c():
+            nc.tensor.matmul(
+                c_ps[:], lhsT=ones[:], rhs=c_row[:].rearrange("p (a t c) -> p a c t", t=TILES, c=PAIR),
+                start=True, stop=True,
+            )
+
+        def load_rows(dst, rows, t0, t1):
+            if t1 - t0 == 1:
+                nc.sync.dma_start(
+                    out=dst[:, 0, :], in_=rows.rearrange("(a t c) f -> t a c f", t=TILES, c=PAIR)[t0]
+                )
+            else:
+                for par in range(PAIR):
+                    nc.sync.dma_start(
+                        out=dst[par:P:PAIR, :, :],
+                        in_=rows.rearrange("(a t c) f -> c a t f", t=TILES, c=PAIR)[par, :, t0:t1, :],
+                    )
+
+        def load_x(g):
+            n0, n1 = x_groups[g]
+            b = n0 // TILES
+            load_rows(x_sb[g], x[b], n0 - TILES * b, n1 - TILES * b)
+
+        def load_rnd(g):
+            load_rows(rnd_sb[g], rnd, *rnd_groups[g])
 
         def load_scales(dst, src):
             for q in range(4):
@@ -71,69 +103,52 @@ def tile_mixturedenserandomsynthesizer_x2_kernel(
                 out=dst[:].bitcast(I32), in_=src[0].rearrange("p n t -> p (n t)").bitcast(I32)
             )
 
-        nc.scalar.dma_start(out=mix_bf[:], in_=mix.partition_broadcast(P))
-        nc.scalar.activation(out=warm[:], in_=warm[:], func=ACT.Exp)
-        nc.sync.dma_start(out=x_sb[0][:, 0:2, :], in_=x_v[0][:, 0:2, :])
-        load_scales(ws_sb, w_scales)
-        nc.sync.dma_start(out=rnd_sb[:, 0:1, :], in_=rnd_v[:, 0:1, :])
-        load_words(w_sb, w_words)
-        nc.sync.dma_start(out=x_sb[0][:, 2:4, :], in_=x_v[0][:, 2:4, :])
-        nc.gpsimd.dma_start(out=rnd_sb[:, 1:2, :], in_=rnd_v[:, 1:2, :])
-        nc.gpsimd.dma_start(out=u_bf[:], in_=u.rearrange("(p t) -> p t", t=TILES))
-        nc.gpsimd.dma_start(out=c_row[0:1, :], in_=c.rearrange("(o k) -> o k", o=1))
-        load_scales(wvs_sb, wv_scales)
-        load_words(wv_sb, wv_words)
-        nc.sync.dma_start(out=rnd_sb[:, 2:4, :], in_=rnd_v[:, 2:4, :])
-        nc.sync.dma_start(out=x_sb[1][:], in_=x_v[1])
-
-        c_ps = psum.tile([P, S], F32, name="c_ps", bufs=1)
+        def in_group(groups, tiles, n):
+            for (n0, n1), tl in zip(groups, tiles):
+                if n0 <= n < n1:
+                    return tl[:, n - n0, :]
 
         def rnd_mix(t, eng):
+            src = in_group(rnd_groups, rnd_sb, t)
             if eng == "v":
                 nc.vector.tensor_scalar(
-                    out=rm[:, t, :], in0=rnd_sb[:, t, :], scalar1=mix_f[:, 1:2], scalar2=None, op0=ALU.mult
+                    out=rm[:, t, :], in0=src, scalar1=mix_f[:, 1:2], scalar2=None, op0=ALU.mult
+                )
+            elif eng == "g":
+                nc.gpsimd.tensor_scalar(
+                    out=rm[:, t, :], in0=src, scalar1=mix_f[:, 1:2], scalar2=0.0, op0=ALU.mult, op1=ALU.add
                 )
             else:
-                nc.scalar.activation(
-                    out=rm[:, t, :], in_=rnd_sb[:, t, :], func=ACT.Copy, scale=mix_f[:, 1:2]
-                )
+                nc.scalar.activation(out=rm[:, t, :], in_=src, func=ACT.Copy, scale=mix_f[:, 1:2])
 
-        xq = [keep.tile([P, S], U32, name="xq%d" % b, align_bytes=64) for b in range(B)]
-        xs = [keep.tile([P, S], U8, name="xs%d" % b, align_bytes=64) for b in range(B)]
-        vg = [keep.tile([P, D, PACK], BF16, name="vg%d" % b, align_bytes=64) for b in range(B)]
-        vq = [keep.tile([P, D], U32, name="vq%d" % b, align_bytes=64) for b in range(B)]
-        vs = [keep.tile([P, D], U8, name="vs%d" % b, align_bytes=64) for b in range(B)]
-        og = [keep.tile([P, S, PACK], BF16, name="og%d" % b, align_bytes=64) for b in range(B)]
-        oq = [keep.tile([P, S], U32, name="oq%d" % b, align_bytes=64) for b in range(B)]
-        os_ = [keep.tile([P, S], U8, name="os%d" % b, align_bytes=64) for b in range(B)]
+        def x_turn(n, cnt):
+            xt = acc_bank()[:].rearrange("p (i h n) -> p i h n", i=2, h=2)
+            for i in range(cnt):
+                words = in_group(x_groups, x_sb, n + i).bitcast(F32)
+                for h in range(2):
+                    nc.tensor.transpose(xt[:, i, h, :], words[:, h : 2 * P : 2], ident[:])
+            state["xt", n] = xt
 
-        state = {}
-
-        def x_turn(n):
-            b, t = divmod(n, TILES)
-            words = x_sb[b][:, t, :].bitcast(F32)
-            xt = psum.tile([P, 2, P], F32, name="turn")
-            for h in range(2):
-                nc.tensor.transpose(xt[:, h, :], words[:, h : 2 * P : 2], ident[:])
-            xg = work.tile([P, P, PACK], BF16, name="xg", align_bytes=64)
+        def x_evac(n, cnt):
+            xg = work.tile([P, 2, P, PACK], BF16, name="xg", align_bytes=64)
             nc.scalar.copy(
-                out=xg[:].rearrange("p n j -> p (n j)").bitcast(F32).rearrange("p (n h) -> p n h", h=2),
-                in_=xt[:].rearrange("p h n -> p n h"),
+                out=xg[:, 0:cnt].rearrange("p i n j -> p (i n j)").bitcast(F32).rearrange("p (i n h) -> p i n h", h=2, i=cnt),
+                in_=state["xt", n][:, 0:cnt].rearrange("p i h n -> p i n h"),
             )
             state["xg", n] = xg
 
-        def x_quant(n):
+        def x_quant(n, cnt):
             b, t = divmod(n, TILES)
-            cols = slice(P * t, P * (t + 1))
+            cols = slice(P * t, P * (t + cnt))
             nc.vector.quantize_mx(
                 out=xq[b][:, cols].bitcast(X4), scales=xs[b][:, cols],
-                in_=state["xg", n][:].rearrange("p n j -> p (n j)"),
+                in_=state["xg", n][:, 0:cnt].rearrange("p i n j -> p (i n j)"),
             )
 
         def syn(n):
             b, t = divmod(n, TILES)
             cols = slice(P * t, P * (t + 1))
-            ps = psum.tile([P, S], F32, name="syn_ps")
+            ps = acc_bank()
             nc.tensor.matmul_mx(
                 out=ps[:], lhsT=xq[b][:, cols].bitcast(X4), lhsT_scale=xs[b][:, cols],
                 rhs=w_sb[:].bitcast(X4), rhs_scale=ws_sb[:], start=True, stop=True,
@@ -141,10 +156,9 @@ def tile_mixturedenserandomsynthesizer_x2_kernel(
             state["syn", n] = ps
 
         def logit(n):
-            t = n % TILES
             lg = work.tile([P, S], F32, name="lg")
             nc.vector.scalar_tensor_tensor(
-                out=lg[:], in0=state["syn", n][:], scalar=mix_f[:, 0:1], in1=rm[:, t, :],
+                out=lg[:], in0=state["syn", n][:], scalar=mix_f[:, 0:1], in1=rm[:, n % TILES, :],
                 op0=ALU.mult, op1=ALU.add,
             )
             state["lg", n] = lg
@@ -160,8 +174,9 @@ def tile_mixturedenserandomsynthesizer_x2_kernel(
             e = work.tile([P, S], F32, name="e")
             tot = work.tile([P, 1], F32, name="tot")
             nc.scalar.activation(
-                out=e[:], in_=state["lg", n][:], func=ACT.Exp, bias=state["nmax", n][:],
-                scale=1.0, accum_out=tot[:],
+                out=e[:].rearrange("p (a c t) -> p a c t", t=TILES, c=PAIR),
+                in_=state["lg", n][:].rearrange("p (a t c) -> p a c t", t=TILES, c=PAIR),
+                func=ACT.Exp, bias=state["nmax", n][:], scale=1.0, accum_out=tot[:],
             )
             state["e", n], state["tot", n] = e, tot
 
@@ -180,67 +195,51 @@ def tile_mixturedenserandomsynthesizer_x2_kernel(
 
         def p_turn(n):
             words = state["pcs", n][:].bitcast(F32)
-            pt = psum.tile([P, 2, P], F32, name="turn")
+            pt = acc_bank()[:].rearrange("p (i h n) -> p i h n", i=2, h=2)
             for h in range(2):
-                nc.tensor.transpose(pt[:, h, :], words[:, h : 2 * P : 2], ident[:])
+                nc.tensor.transpose(pt[:, 0, h, :], words[:, h : 2 * P : 2], ident[:])
             state["pt", n] = pt
 
         def p_evac(n):
             pg = work.tile([P, P, PACK], BF16, name="pg", align_bytes=64)
             nc.scalar.copy(
                 out=pg[:].rearrange("p n j -> p (n j)").bitcast(F32).rearrange("p (n h) -> p n h", h=2),
-                in_=state["pt", n][:].rearrange("p h n -> p n h"),
+                in_=state["pt", n][:, 0].rearrange("p h n -> p n h"),
             )
             state["pg", n] = pg
 
         def p_quant(n):
-            pq = work.tile([P, P], U32, name="pq", align_bytes=64)
-            pqs = work.tile([P, P], U8, name="pqs", align_bytes=64)
             nc.vector.quantize_mx(
-                out=pq[:].bitcast(X4), scales=pqs[:],
+                out=pq[n][:].bitcast(X4), scales=pqs[n][:],
                 in_=state["pg", n][:].rearrange("p n j -> p (n j)"),
             )
-            state["pq", n] = (pq, pqs)
 
-        def v_mm(i):
-            b, ch = divmod(i, TILES)
-            ps = psum.tile([P, PACK, P], F32, name="quad_ps")
-            dcols = slice(P * ch, P * (ch + 1))
-            for t in range(PACK):
-                cols = slice(P * t, P * (t + 1))
-                nc.tensor.matmul_mx(
-                    out=ps[:, t, :], lhsT=xq[b][:, cols].bitcast(X4), lhsT_scale=xs[b][:, cols],
-                    rhs=wv_sb[:, dcols].bitcast(X4), rhs_scale=wvs_sb[:, dcols], start=True, stop=True,
-                )
-            state["vps", i] = ps
+        def acc_bank():
+            acc = psum.tile([P, D], F32, name="acc", bufs=7)
+            return acc
 
-        def v_gain(i):
-            b, ch = divmod(i, TILES)
-            m = P // PACK
-            nc.vector.tensor_tensor(
-                out=vg[b][:].rearrange("p (d m) t -> p d m t", d=PACK)[:, :, m * ch : m * (ch + 1), :],
-                in0=state["vps", i][:].rearrange("p t (m d) -> p d m t", d=PACK),
-                in1=u_bf[:].unsqueeze(1).unsqueeze(1).to_broadcast([P, PACK, m, PACK]),
-                op=ALU.mult,
-            )
-
-        def v0_slot(t):
+        def v_mm(n):
+            b, t = divmod(n, TILES)
             cols = slice(P * t, P * (t + 1))
-            ps = psum.tile([P, D], F32, name="quad_ps")
+            ps = acc_bank()
             nc.tensor.matmul_mx(
-                out=ps[:], lhsT=xq[0][:, cols].bitcast(X4), lhsT_scale=xs[0][:, cols],
+                out=ps[:], lhsT=xq[b][:, cols].bitcast(X4), lhsT_scale=xs[b][:, cols],
                 rhs=wv_sb[:].bitcast(X4), rhs_scale=wvs_sb[:], start=True, stop=True,
             )
+            state["vps", n] = ps
+
+        def v_gain(n):
+            b, t = divmod(n, TILES)
             nc.scalar.activation(
-                out=vn[:, t, :].rearrange("p (d m) -> p d m", d=PACK),
-                in_=ps[:].rearrange("p (m d) -> p d m", d=PACK),
+                out=vn[b][:, t, :].rearrange("p (d m) -> p d m", d=PACK),
+                in_=state["vps", n][:].rearrange("p (m d) -> p d m", d=PACK),
                 func=ACT.Copy, scale=u_f[:, t : t + 1],
             )
 
-        def v0_pack():
+        def v_pack(b, c0, c1):
             nc.vector.tensor_copy(
-                out=vg[0][:].rearrange("p (c i) t -> p c t i", i=PACK),
-                in_=vn[:].rearrange("p t (c i) -> p c t i", i=PACK),
+                out=vg[b][:, c0:c1, :].rearrange("p (c i) t -> p c t i", i=PACK),
+                in_=vn[b][:, :, c0:c1].rearrange("p t (c i) -> p c t i", i=PACK),
             )
 
         def v_quant(b):
@@ -248,54 +247,47 @@ def tile_mixturedenserandomsynthesizer_x2_kernel(
                 out=vq[b][:].bitcast(X4), scales=vs[b][:], in_=vg[b][:].rearrange("p n j -> p (n j)")
             )
 
-        def nat_mm(nat, n):
+        def nat_mm(n):
             b = n // TILES
-            pq, pqs = state["pq", n]
+            nat = acc_bank()
             nc.tensor.matmul_mx(
-                out=nat[:], lhsT=pq[:].bitcast(X4), lhsT_scale=pqs[:],
+                out=nat[:], lhsT=pq[n][:].bitcast(X4), lhsT_scale=pqs[n][:],
                 rhs=vq[b][:].bitcast(X4), rhs_scale=vs[b][:], start=True, stop=True,
             )
+            state["nat", n] = nat
 
-        def out_mm(n):
+        def quad_mm(n, p0, p1):
             b = n // TILES
-            pq, pqs = state["pq", n]
-            qd = psum.tile([P, PACK, P], F32, name="quad_ps")
-            if n == N_TILES - 1:
-                nat = psum.tile([P, D], F32, name="syn_ps")
-                nat_mm(nat, n)
+            qd = acc_bank()
+            w = p1 - p0
             for d in range(PACK):
                 cols = slice(P * d, P * (d + 1))
                 nc.tensor.matmul_mx(
-                    out=qd[:, d, :], lhsT=vq[b][:, cols].bitcast(X4), lhsT_scale=vs[b][:, cols],
-                    rhs=pq[:].bitcast(X4), rhs_scale=pqs[:], start=True, stop=True,
+                    out=qd[:, w * d : w * (d + 1)], lhsT=vq[b][:, cols].bitcast(X4), lhsT_scale=vs[b][:, cols],
+                    rhs=pq[n][:, p0:p1].bitcast(X4), rhs_scale=pqs[n][:, p0:p1], start=True, stop=True,
                 )
-            if n < N_TILES - 1:
-                if n == N_TILES - 3:
-                    nat = psum.tile([P, D], F32, name="syn_ps")
-                else:
-                    nat = psum.tile([P, D], F32, name="nat_ps", bufs=1)
-                nat_mm(nat, n)
-            state["qd", n], state["nat", n] = qd, nat
+            state["qd", n, p0] = qd
+
+        def copier(eng):
+            return nc.scalar.copy if eng == "s" else nc.vector.tensor_copy
 
         def nat_evac(n, eng):
-            ob = work.tile([P, D], F32, name="ob")
-            state["ob", n] = ob
-            src = state["nat", n][:].rearrange("p (d m) -> p m d", d=PACK)
-            dst = ob[:].rearrange("p (m d) -> p m d", d=PACK)
-            if eng == "s":
-                nc.scalar.copy(out=dst, in_=src)
-            else:
-                nc.vector.tensor_copy(out=dst, in_=src)
-
-        def nat_store(n, eng):
             b, t = divmod(n, TILES)
-            eng.dma_start(out=out_0[b].rearrange("(p t) d -> p t d", t=TILES)[:, t, :], in_=state["ob", n][:])
+            ob = work.tile([P, D], F32, name="ob")
+            copier(eng)(
+                out=ob[:].rearrange("p (m d) -> p m d", d=PACK),
+                in_=state["nat", n][:].rearrange("p (d m) -> p m d", d=PACK),
+            )
+            nc.sync.dma_start(
+                out=out_0[b].rearrange("(a t c) d -> t a c d", t=TILES, c=PAIR)[t], in_=ob[:]
+            )
 
         def quad_evac(n, p0, p1, eng):
             b, t = divmod(n, TILES)
-            (nc.scalar.copy if eng == "s" else nc.vector.tensor_copy)(
-                out=og[b][:].rearrange("m (p t) d -> m t p d", t=TILES)[:, t, p0:p1, :],
-                in_=state["qd", n][:].rearrange("m d p -> m p d")[:, p0:p1, :],
+            w = p1 - p0
+            copier(eng)(
+                out=og[b][:].rearrange("m (a t c) d -> m t a c d", t=TILES, c=PAIR)[:, t, p0 // PAIR : p1 // PAIR],
+                in_=state["qd", n, p0][:, 0 : PACK * w].rearrange("m (d a c) -> m a c d", d=PACK, c=PAIR),
             )
 
         def o_quant(b, i0, i1):
@@ -303,8 +295,6 @@ def tile_mixturedenserandomsynthesizer_x2_kernel(
                 out=oq[b][:, i0:i1].bitcast(X4), scales=os_[b][:, i0:i1],
                 in_=og[b][:, i0:i1, :].rearrange("m i d -> m (i d)"),
             )
-
-        def o_store(b, i0, i1):
             nc.sync.dma_start(
                 out=out_1[0][:, S * b + i0 : S * b + i1, :].rearrange("m i d -> m (i d)").bitcast(I32),
                 in_=oq[b][:, i0:i1].bitcast(I32),
@@ -317,116 +307,177 @@ def tile_mixturedenserandomsynthesizer_x2_kernel(
                     in_=os_[b][32 * q : 32 * q + 4, :].bitcast(I32),
                 )
 
-        V_CHUNKS = {4: [4], 5: [5], 6: [6, 7]}
-        X_AHEAD = {3: [4, 5, 6, 7]}
-        LAST = N_TILES - 1
+        nc.vector.memset(ws_sb[:].bitcast(I32), 0)
+        nc.vector.memset(wvs_sb[:].bitcast(I32), 0)
+        nc.vector.memset(c_row[:], 0.0)
+        nc.vector.memset(ones[:], 1.0)
+        make_identity(nc, ident[:])
+        nc.scalar.dma_start(out=mix_bf[:], in_=mix.partition_broadcast(P))
+        load_x(0)
+        load_x(1)
+        load_words(w_sb, w_words)
+        load_scales(ws_sb, w_scales)
+        for par in range(PAIR):
+            nc.gpsimd.dma_start(
+                out=u_bf[par:P:PAIR, 0:7], in_=u.rearrange("(a j) -> a j", j=8)[:, par : par + 7]
+            )
+        load_rnd(0)
+        load_rnd(1)
+        load_x(2)
+        load_rnd(2)
+        load_words(wv_sb, wv_words)
+        nc.sync.dma_start(out=c_row[0:1, :], in_=c.rearrange("(o k) -> o k", o=1))
+        load_scales(wvs_sb, wv_scales)
+        load_x(3)
 
-        def live(n):
-            return 0 <= n < N_TILES
-
-        def body():
-            x_turn(0)
-            x_turn(1)
-            nc.vector.tensor_copy(out=mix_f[:], in_=mix_bf[:])
-            rnd_mix(1, "s")
-            x_quant(0)
-            syn(0)
-            rnd_mix(0, "v")
-            x_quant(1)
-            syn(1)
-            logit(0)
-            x_turn(2)
-            x_turn(3)
-            row_max(0)
-            expo(0)
-            x_quant(2)
-            x_quant(3)
-            nc.vector.tensor_copy(out=u_f[:], in_=u_bf[:])
-            v0_slot(0)
-            v0_slot(1)
-            nc.tensor.matmul(c_ps[:], lhsT=ones[:], rhs=c_row[:], start=True, stop=True)
-            for k in range(1, N_TILES):
-                if live(k - 2):
-                    p_turn(k - 2)
-                if live(k - 3):
-                    out_mm(k - 3)
-                logit(k)
-                recip(k - 1)
-                if live(k - 2):
-                    p_evac(k - 2)
-                if live(k - 3):
-                    quad_evac(k - 3, 0, P, "s")
-                for n in X_AHEAD.get(k, []):
-                    x_quant(n)
-                for i in V_CHUNKS.get(k, [])[:1]:
-                    v_gain(i)
-                if k == 1:
-                    rnd_mix(2, "v")
-                if k == 2:
-                    rnd_mix(3, "v")
-                if k == LAST:
-                    p_quant(k - 2)
-                    pc(k - 1)
-                row_max(k)
-                expo(k)
-                if k == 2:
-                    v0_pack()
-                for i in V_CHUNKS.get(k, [])[1:]:
-                    v_mm(i)
-                    v_gain(i)
-                if k == LAST:
-                    break
-                if live(k - 3):
-                    nat_evac(k - 3, "s")
-                    nat_store(k - 3, nc.sync)
-                if live(k - 2):
-                    p_quant(k - 2)
-                if k == 2:
-                    v_quant(0)
-                pc(k - 1)
-                if k == LAST - 1:
-                    v_quant(1)
-                if live(k + 1):
-                    syn(k + 1)
-                if k == 1:
-                    v0_slot(2)
-                    v0_slot(3)
-                for n in X_AHEAD.get(k + 1, []):
-                    x_turn(n)
-                for i in V_CHUNKS.get(k + 1, [])[:1]:
-                    v_mm(i)
-            p_turn(LAST - 1)
-            out_mm(LAST - 2)
-            o_quant(0, 0, S)
-            o_store(0, 0, S)
-            o_scales(0)
-            recip(LAST)
-            p_evac(LAST - 1)
-            pc(LAST)
-            nat_evac(LAST - 3, "s")
-            nat_store(LAST - 3, nc.sync)
-            nat_evac(LAST - 2, "s")
-            nat_store(LAST - 2, nc.sync)
-            p_turn(LAST)
-            p_quant(LAST - 1)
-            out_mm(LAST - 1)
-            p_evac(LAST)
-            quad_evac(LAST - 2, 0, P, "v")
-            p_quant(LAST)
-            quad_evac(LAST - 1, 0, P, "s")
-            out_mm(LAST)
-            nat_evac(LAST - 1, "v")
-            nat_store(LAST - 1, nc.sync)
-            nat_evac(LAST, "v")
-            nat_store(LAST, nc.sync)
-            quad_evac(LAST, 0, P // 2, "s")
-            quad_evac(LAST, P // 2, P, "s")
-            o_quant(1, 0, S // 2)
-            o_store(1, 0, S // 2)
-            o_quant(1, S // 2, S)
-            o_store(1, S // 2, S)
-            o_scales(1)
-
-        if MANUAL_ORDER:
-            ctx.enter_context(tc.manual_schedule())
-        body()
+        nc.scalar.activation(out=mix_f[:], in_=mix_bf[:], func=ACT.Copy)
+        x_turn(0, 1)
+        x_turn(1, 1)
+        x_evac(0, 1)
+        x_evac(1, 1)
+        x_quant(0, 1)
+        syn(0)
+        x_quant(1, 1)
+        rnd_mix(0, "v")
+        syn(1)
+        nc.vector.tensor_copy(out=u_f[:], in_=u_bf[:, 0:7:2])
+        x_turn(2, 2)
+        rnd_mix(1, "s")
+        rnd_mix(2, "s")
+        v_mm(0)
+        v_mm(1)
+        spread_c()
+        logit(0)
+        logit(1)
+        x_evac(2, 2)
+        row_max(0)
+        x_quant(2, 2)
+        syn(2)
+        syn(3)
+        v_mm(2)
+        v_mm(3)
+        x_turn(4, 2)
+        x_turn(6, 2)
+        expo(0)
+        row_max(1)
+        expo(1)
+        rnd_mix(3, "v")
+        recip(0)
+        logit(2)
+        v_gain(0)
+        v_gain(1)
+        pc(0)
+        p_turn(0)
+        row_max(2)
+        x_evac(4, 2)
+        v_gain(2)
+        v_gain(3)
+        recip(1)
+        logit(3)
+        x_quant(4, 2)
+        syn(4)
+        v_mm(4)
+        v_mm(5)
+        syn(5)
+        p_evac(0)
+        expo(2)
+        x_evac(6, 2)
+        pc(1)
+        p_turn(1)
+        row_max(3)
+        p_quant(0)
+        v_pack(0, 0, D)
+        x_quant(6, 2)
+        v_mm(6)
+        v_mm(7)
+        recip(2)
+        logit(4)
+        p_evac(1)
+        expo(3)
+        v_gain(4)
+        v_gain(5)
+        pc(2)
+        p_turn(2)
+        syn(6)
+        row_max(4)
+        p_quant(1)
+        v_quant(0)
+        v_gain(6)
+        v_gain(7)
+        quad_mm(0, 0, P)
+        nat_mm(0)
+        quad_mm(1, 0, P)
+        recip(3)
+        logit(5)
+        p_evac(2)
+        expo(4)
+        pc(3)
+        p_turn(3)
+        nat_mm(1)
+        syn(7)
+        row_max(5)
+        p_quant(2)
+        quad_evac(0, 0, P, "s")
+        nat_evac(0, "s")
+        quad_mm(2, 0, P)
+        quad_evac(1, 0, P, "s")
+        v_pack(1, 0, D)
+        recip(4)
+        logit(6)
+        p_evac(3)
+        expo(5)
+        pc(4)
+        nat_mm(2)
+        p_turn(4)
+        row_max(6)
+        p_quant(3)
+        nat_evac(1, "s")
+        quad_mm(3, 0, P)
+        quad_evac(2, 0, P, "s")
+        nat_evac(2, "s")
+        recip(5)
+        logit(7)
+        p_evac(4)
+        expo(6)
+        pc(5)
+        p_turn(5)
+        nat_mm(3)
+        row_max(7)
+        p_quant(4)
+        quad_evac(3, 0, P, "s")
+        expo(7)
+        recip(6)
+        v_quant(1)
+        quad_mm(4, 0, P)
+        p_evac(5)
+        pc(6)
+        p_turn(6)
+        nat_mm(4)
+        nat_evac(3, "s")
+        recip(7)
+        p_quant(5)
+        quad_evac(4, 0, P, "s")
+        pc(7)
+        p_turn(7)
+        quad_mm(5, 0, P)
+        nat_mm(5)
+        p_evac(6)
+        o_quant(0, 0, S)
+        o_scales(0)
+        p_evac(7)
+        p_quant(6)
+        quad_mm(6, 0, P)
+        nat_evac(4, "v")
+        p_quant(7)
+        quad_mm(7, 0, P)
+        nat_mm(6)
+        nat_mm(7)
+        quad_evac(5, 0, P, "s")
+        nat_evac(5, "v")
+        quad_evac(6, 0, P, "s")
+        quad_evac(7, 0, P, "v")
+        nat_evac(6, "s")
+        o_quant(1, 0, S // 2)
+        o_quant(1, S // 2, S)
+        nat_evac(7, "s")
+        o_scales(1)

@@ -43,7 +43,6 @@ def tile_mixturedenserandomsynthesizer_x2_kernel(
         wvs_sb = keep.tile([P, D], U8, name="wvs_sb", align_bytes=64)
         rm = keep.tile([P, TILES, S], F32, name="rm")
         mix_bf = keep.tile([P, 2], BF16, name="mix_bf")
-        mix_f = keep.tile([P, 2], F32, name="mix_f")
         u_bf = keep.tile([P, 8], BF16, name="u_bf")
         u_f = keep.tile([P, TILES], F32, name="u_f")
         c_row = keep.tile([P, S], BF16, name="c_row")
@@ -60,8 +59,12 @@ def tile_mixturedenserandomsynthesizer_x2_kernel(
         og = [keep.tile([P, S, PACK], BF16, name="og%d" % b, align_bytes=64) for b in range(B)]
         oq = [keep.tile([P, S], U32, name="oq%d" % b, align_bytes=64) for b in range(B)]
         os_ = [keep.tile([P, S], U8, name="os%d" % b, align_bytes=64) for b in range(B)]
-        pq = [keep.tile([P, P], U32, name="pq%d" % n, align_bytes=64) for n in range(N_TILES)]
-        pqs = [keep.tile([P, P], U8, name="pqs%d" % n, align_bytes=64) for n in range(N_TILES)]
+        pq = keep.tile([P, N_TILES * P], U32, name="pq", align_bytes=64)
+        pqs = keep.tile([P, N_TILES * P], U8, name="pqs", align_bytes=64)
+        lg = keep.tile([P, N_TILES, S], F32, name="lg")
+        nmax = keep.tile([P, N_TILES], F32, name="nmax")
+        tot = keep.tile([P, N_TILES], F32, name="tot")
+        rinv = keep.tile([P, N_TILES], F32, name="rinv")
 
         state = {}
 
@@ -112,14 +115,12 @@ def tile_mixturedenserandomsynthesizer_x2_kernel(
             src = in_group(rnd_groups, rnd_sb, t)
             if eng == "v":
                 nc.vector.tensor_scalar(
-                    out=rm[:, t, :], in0=src, scalar1=mix_f[:, 1:2], scalar2=None, op0=ALU.mult
-                )
-            elif eng == "g":
-                nc.gpsimd.tensor_scalar(
-                    out=rm[:, t, :], in0=src, scalar1=mix_f[:, 1:2], scalar2=0.0, op0=ALU.mult, op1=ALU.add
+                    out=rm[:, t, :], in0=src, scalar1=mix_bf[:, 1:2], scalar2=None, op0=ALU.mult
                 )
             else:
-                nc.scalar.activation(out=rm[:, t, :], in_=src, func=ACT.Copy, scale=mix_f[:, 1:2])
+                nc.gpsimd.tensor_scalar(
+                    out=rm[:, t, :], in0=src, scalar1=mix_bf[:, 1:2], scalar2=0.0, op0=ALU.mult, op1=ALU.add
+                )
 
         def x_turn(n, cnt):
             xt = acc_bank()[:].rearrange("p (i h n) -> p i h n", i=2, h=2)
@@ -156,62 +157,57 @@ def tile_mixturedenserandomsynthesizer_x2_kernel(
             state["syn", n] = ps
 
         def logit(n):
-            lg = work.tile([P, S], F32, name="lg")
             nc.vector.scalar_tensor_tensor(
-                out=lg[:], in0=state["syn", n][:], scalar=mix_f[:, 0:1], in1=rm[:, n % TILES, :],
+                out=lg[:, n, :], in0=state["syn", n][:], scalar=mix_bf[:, 0:1], in1=rm[:, n % TILES, :],
                 op0=ALU.mult, op1=ALU.add,
             )
-            state["lg", n] = lg
 
-        def row_max(n):
-            nmax = work.tile([P, 1], F32, name="nmax")
+        def row_max(n, cnt):
             nc.vector.tensor_reduce(
-                out=nmax[:], in_=state["lg", n][:], axis=AXIS.X, op=ALU.max, negate=True
+                out=nmax[:, n : n + cnt], in_=lg[:, n : n + cnt, :], axis=AXIS.X, op=ALU.max, negate=True
             )
-            state["nmax", n] = nmax
 
         def expo(n):
             e = work.tile([P, S], F32, name="e")
-            tot = work.tile([P, 1], F32, name="tot")
             nc.scalar.activation(
                 out=e[:].rearrange("p (a c t) -> p a c t", t=TILES, c=PAIR),
-                in_=state["lg", n][:].rearrange("p (a t c) -> p a c t", t=TILES, c=PAIR),
-                func=ACT.Exp, bias=state["nmax", n][:], scale=1.0, accum_out=tot[:],
+                in_=lg[:, n, :].rearrange("p (a t c) -> p a c t", t=TILES, c=PAIR),
+                func=ACT.Exp, bias=nmax[:, n : n + 1], scale=1.0, accum_out=tot[:, n : n + 1],
             )
-            state["e", n], state["tot", n] = e, tot
+            state["e", n] = e
 
-        def recip(n):
-            rinv = work.tile([P, 1], F32, name="rinv")
-            nc.vector.reciprocal(rinv[:], state["tot", n][:])
-            state["rinv", n] = rinv
+        def recip(n, cnt):
+            nc.vector.reciprocal(rinv[:, n : n + cnt], tot[:, n : n + cnt])
 
         def pc(n):
             pcs = work.tile([P, S], BF16, name="pcs", align_bytes=64)
             nc.vector.scalar_tensor_tensor(
-                out=pcs[:], in0=state["e", n][:], scalar=state["rinv", n][:], in1=c_ps[:],
+                out=pcs[:], in0=state["e", n][:], scalar=rinv[:, n : n + 1], in1=c_ps[:],
                 op0=ALU.mult, op1=ALU.mult,
             )
             state["pcs", n] = pcs
 
-        def p_turn(n):
-            words = state["pcs", n][:].bitcast(F32)
+        def p_turn(n, cnt):
             pt = acc_bank()[:].rearrange("p (i h n) -> p i h n", i=2, h=2)
-            for h in range(2):
-                nc.tensor.transpose(pt[:, 0, h, :], words[:, h : 2 * P : 2], ident[:])
+            for i in range(cnt):
+                words = state["pcs", n + i][:].bitcast(F32)
+                for h in range(2):
+                    nc.tensor.transpose(pt[:, i, h, :], words[:, h : 2 * P : 2], ident[:])
             state["pt", n] = pt
 
-        def p_evac(n):
-            pg = work.tile([P, P, PACK], BF16, name="pg", align_bytes=64)
+        def p_evac(n, cnt):
+            pg = work.tile([P, 2, P, PACK], BF16, name="pg", align_bytes=64)
             nc.scalar.copy(
-                out=pg[:].rearrange("p n j -> p (n j)").bitcast(F32).rearrange("p (n h) -> p n h", h=2),
-                in_=state["pt", n][:, 0].rearrange("p h n -> p n h"),
+                out=pg[:, 0:cnt].rearrange("p i n j -> p (i n j)").bitcast(F32).rearrange("p (i n h) -> p i n h", h=2, i=cnt),
+                in_=state["pt", n][:, 0:cnt].rearrange("p i h n -> p i n h"),
             )
             state["pg", n] = pg
 
-        def p_quant(n):
+        def p_quant(n, cnt):
+            cols = slice(P * n, P * (n + cnt))
             nc.vector.quantize_mx(
-                out=pq[n][:].bitcast(X4), scales=pqs[n][:],
-                in_=state["pg", n][:].rearrange("p n j -> p (n j)"),
+                out=pq[:, cols].bitcast(X4), scales=pqs[:, cols],
+                in_=state["pg", n][:, 0:cnt].rearrange("p i n j -> p (i n j)"),
             )
 
         def acc_bank():
@@ -242,6 +238,14 @@ def tile_mixturedenserandomsynthesizer_x2_kernel(
                 in_=vn[b][:, :, c0:c1].rearrange("p t (c i) -> p c t i", i=PACK),
             )
 
+        def v_pack_g(b, pieces):
+            w = D // pieces
+            for c0 in range(0, D, w):
+                nc.gpsimd.tensor_scalar(
+                    out=vg[b][:, c0 : c0 + w, :], in0=vn[b][:, :, c0 : c0 + w].rearrange("p t c -> p c t"),
+                    scalar1=1.0, scalar2=0.0, op0=ALU.mult, op1=ALU.add,
+                )
+
         def v_quant(b):
             nc.vector.quantize_mx(
                 out=vq[b][:].bitcast(X4), scales=vs[b][:], in_=vg[b][:].rearrange("p n j -> p (n j)")
@@ -251,7 +255,7 @@ def tile_mixturedenserandomsynthesizer_x2_kernel(
             b = n // TILES
             nat = acc_bank()
             nc.tensor.matmul_mx(
-                out=nat[:], lhsT=pq[n][:].bitcast(X4), lhsT_scale=pqs[n][:],
+                out=nat[:], lhsT=pq[:, P * n : P * (n + 1)].bitcast(X4), lhsT_scale=pqs[:, P * n : P * (n + 1)],
                 rhs=vq[b][:].bitcast(X4), rhs_scale=vs[b][:], start=True, stop=True,
             )
             state["nat", n] = nat
@@ -264,7 +268,7 @@ def tile_mixturedenserandomsynthesizer_x2_kernel(
                 cols = slice(P * d, P * (d + 1))
                 nc.tensor.matmul_mx(
                     out=qd[:, w * d : w * (d + 1)], lhsT=vq[b][:, cols].bitcast(X4), lhsT_scale=vs[b][:, cols],
-                    rhs=pq[n][:, p0:p1].bitcast(X4), rhs_scale=pqs[n][:, p0:p1], start=True, stop=True,
+                    rhs=pq[:, P * n + p0 : P * n + p1].bitcast(X4), rhs_scale=pqs[:, P * n + p0 : P * n + p1], start=True, stop=True,
                 )
             state["qd", n, p0] = qd
 
@@ -300,37 +304,36 @@ def tile_mixturedenserandomsynthesizer_x2_kernel(
                 in_=oq[b][:, i0:i1].bitcast(I32),
             )
 
-        def o_scales(b):
+        def o_scales(b, queues):
             for q in range(4):
-                nc.sync.dma_start(
+                queues[q].dma_start(
                     out=out_2[0, 4 * q : 4 * q + 4, S * b : S * (b + 1)].bitcast(I32),
                     in_=os_[b][32 * q : 32 * q + 4, :].bitcast(I32),
                 )
 
         nc.vector.memset(ws_sb[:].bitcast(I32), 0)
-        nc.vector.memset(wvs_sb[:].bitcast(I32), 0)
         nc.vector.memset(c_row[:], 0.0)
-        nc.vector.memset(ones[:], 1.0)
+        nc.vector.memset(wvs_sb[:].bitcast(I32), 0)
+        nc.scalar.activation(out=ones[:], in_=c_row[:, 0:P], func=ACT.Copy, bias=1.0)
+        nc.gpsimd.dma_start(out=mix_bf[:], in_=mix.partition_broadcast(P))
         make_identity(nc, ident[:])
-        nc.scalar.dma_start(out=mix_bf[:], in_=mix.partition_broadcast(P))
         load_x(0)
         load_x(1)
         load_words(w_sb, w_words)
+        load_rnd(0)
         load_scales(ws_sb, w_scales)
         for par in range(PAIR):
             nc.gpsimd.dma_start(
                 out=u_bf[par:P:PAIR, 0:7], in_=u.rearrange("(a j) -> a j", j=8)[:, par : par + 7]
             )
-        load_rnd(0)
         load_rnd(1)
-        load_x(2)
-        load_rnd(2)
         load_words(wv_sb, wv_words)
-        nc.sync.dma_start(out=c_row[0:1, :], in_=c.rearrange("(o k) -> o k", o=1))
+        load_x(2)
         load_scales(wvs_sb, wv_scales)
+        load_rnd(2)
+        nc.sync.dma_start(out=c_row[0:1, :], in_=c.rearrange("(o k) -> o k", o=1))
         load_x(3)
 
-        nc.scalar.activation(out=mix_f[:], in_=mix_bf[:], func=ACT.Copy)
         x_turn(0, 1)
         x_turn(1, 1)
         x_evac(0, 1)
@@ -340,17 +343,19 @@ def tile_mixturedenserandomsynthesizer_x2_kernel(
         x_quant(1, 1)
         rnd_mix(0, "v")
         syn(1)
-        nc.vector.tensor_copy(out=u_f[:], in_=u_bf[:, 0:7:2])
+        rnd_mix(1, "v")
+        nc.gpsimd.tensor_copy(out=u_f[:], in_=u_bf[:, 0:7:2])
         x_turn(2, 2)
-        rnd_mix(1, "s")
-        rnd_mix(2, "s")
         v_mm(0)
         v_mm(1)
         spread_c()
         logit(0)
         logit(1)
         x_evac(2, 2)
-        row_max(0)
+        row_max(0, 1)
+        expo(0)
+        v_gain(0)
+        row_max(1, 1)
         x_quant(2, 2)
         syn(2)
         syn(3)
@@ -358,126 +363,123 @@ def tile_mixturedenserandomsynthesizer_x2_kernel(
         v_mm(3)
         x_turn(4, 2)
         x_turn(6, 2)
-        expo(0)
-        row_max(1)
         expo(1)
-        rnd_mix(3, "v")
-        recip(0)
-        logit(2)
-        v_gain(0)
         v_gain(1)
+        rnd_mix(2, "v")
+        recip(0, 1)
+        rnd_mix(3, "v")
         pc(0)
-        p_turn(0)
-        row_max(2)
-        x_evac(4, 2)
+        p_turn(0, 1)
         v_gain(2)
         v_gain(3)
-        recip(1)
+        v_pack_g(0, 4)
+        x_evac(4, 2)
+        p_evac(0, 1)
+        x_evac(6, 2)
+        logit(2)
         logit(3)
+        recip(1, 1)
+        row_max(2, 1)
+        pc(1)
+        p_turn(1, 1)
         x_quant(4, 2)
         syn(4)
         v_mm(4)
         v_mm(5)
         syn(5)
-        p_evac(0)
         expo(2)
-        x_evac(6, 2)
-        pc(1)
-        p_turn(1)
-        row_max(3)
-        p_quant(0)
-        v_pack(0, 0, D)
+        p_evac(1, 1)
+        row_max(3, 1)
+        expo(3)
         x_quant(6, 2)
         v_mm(6)
         v_mm(7)
-        recip(2)
+        p_quant(0, 1)
+        recip(2, 1)
         logit(4)
-        p_evac(1)
-        expo(3)
         v_gain(4)
         v_gain(5)
-        pc(2)
-        p_turn(2)
-        syn(6)
-        row_max(4)
-        p_quant(1)
-        v_quant(0)
         v_gain(6)
         v_gain(7)
-        quad_mm(0, 0, P)
+        v_pack_g(1, 4)
+        pc(2)
+        p_turn(2, 1)
+        syn(6)
+        row_max(4, 1)
+        p_quant(1, 1)
+        v_quant(0)
         nat_mm(0)
-        quad_mm(1, 0, P)
-        recip(3)
-        logit(5)
-        p_evac(2)
-        expo(4)
-        pc(3)
-        p_turn(3)
+        quad_mm(0, 0, P)
         nat_mm(1)
+        expo(4)
+        p_evac(2, 1)
+        recip(3, 1)
+        logit(5)
+        pc(3)
+        p_turn(3, 1)
         syn(7)
-        row_max(5)
-        p_quant(2)
-        quad_evac(0, 0, P, "s")
+        quad_mm(1, 0, P)
+        row_max(5, 1)
+        p_quant(2, 1)
         nat_evac(0, "s")
-        quad_mm(2, 0, P)
-        quad_evac(1, 0, P, "s")
-        v_pack(1, 0, D)
-        recip(4)
-        logit(6)
-        p_evac(3)
-        expo(5)
-        pc(4)
+        quad_evac(0, 0, P, "s")
         nat_mm(2)
-        p_turn(4)
-        row_max(6)
-        p_quant(3)
-        nat_evac(1, "s")
-        quad_mm(3, 0, P)
-        quad_evac(2, 0, P, "s")
-        nat_evac(2, "s")
-        recip(5)
-        logit(7)
-        p_evac(4)
-        expo(6)
-        pc(5)
-        p_turn(5)
+        expo(5)
+        p_evac(3, 1)
+        recip(4, 1)
+        logit(6)
+        pc(4)
+        p_turn(4, 1)
+        quad_mm(2, 0, P)
+        row_max(6, 1)
+        p_quant(3, 1)
         nat_mm(3)
-        row_max(7)
-        p_quant(4)
-        quad_evac(3, 0, P, "s")
+        nat_evac(1, "s")
+        quad_evac(1, 0, P, "s")
+        nat_evac(2, "s")
+        expo(6)
+        p_evac(4, 1)
+        recip(5, 1)
+        logit(7)
+        pc(5)
+        p_turn(5, 1)
+        quad_mm(3, 0, P)
+        row_max(7, 1)
+        p_quant(4, 1)
+        quad_evac(2, 0, P, "s")
         expo(7)
-        recip(6)
+        p_evac(5, 1)
+        recip(6, 1)
         v_quant(1)
-        quad_mm(4, 0, P)
-        p_evac(5)
-        pc(6)
-        p_turn(6)
         nat_mm(4)
+        pc(6)
+        p_turn(6, 1)
+        quad_mm(4, 0, P)
+        recip(7, 1)
+        p_quant(5, 1)
         nat_evac(3, "s")
-        recip(7)
-        p_quant(5)
-        quad_evac(4, 0, P, "s")
+        quad_evac(3, 0, P, "s")
         pc(7)
-        p_turn(7)
-        quad_mm(5, 0, P)
+        p_turn(7, 1)
         nat_mm(5)
-        p_evac(6)
+        quad_mm(5, 0, P)
+        p_evac(6, 1)
         o_quant(0, 0, S)
-        o_scales(0)
-        p_evac(7)
-        p_quant(6)
-        quad_mm(6, 0, P)
-        nat_evac(4, "v")
-        p_quant(7)
-        quad_mm(7, 0, P)
+        o_scales(0, [nc.sync] * 4)
+        nat_evac(4, "s")
+        p_evac(7, 1)
+        p_quant(6, 1)
         nat_mm(6)
+        quad_mm(6, 0, P)
+        quad_evac(4, 0, P, "v")
+        p_quant(7, 1)
+        quad_mm(7, 0, P)
         nat_mm(7)
-        quad_evac(5, 0, P, "s")
-        nat_evac(5, "v")
+        nat_evac(5, "s")
+        quad_evac(5, 0, P, "v")
+        nat_evac(6, "s")
         quad_evac(6, 0, P, "s")
         quad_evac(7, 0, P, "v")
-        nat_evac(6, "s")
-        o_quant(1, 0, S // 2)
-        o_quant(1, S // 2, S)
         nat_evac(7, "s")
-        o_scales(1)
+        o_quant(1, 0, S)
+        o_scales(1, [nc.sync, nc.scalar, nc.sync, nc.scalar])

@@ -21,6 +21,8 @@ PACK = 4
 TILES = S // P
 N_TILES = B * TILES
 PAIR = 2
+HALF = D // 2
+SHARES = {("v", 0, 0): ("x", 6), ("v", 0, 1): ("p", 0), ("v", 1, 0): ("p", 1), ("v", 1, 1): ("p", 3)}
 
 
 def tile_mixturedenserandomsynthesizer_x2_kernel(
@@ -53,7 +55,6 @@ def tile_mixturedenserandomsynthesizer_x2_kernel(
         xq = [keep.tile([P, S], U32, name="xq%d" % b, align_bytes=64) for b in range(B)]
         xs = [keep.tile([P, S], U8, name="xs%d" % b, align_bytes=64) for b in range(B)]
         vn = [keep.tile([P, PACK, D], BF16, name="vn%d" % b, align_bytes=64) for b in range(B)]
-        vg = [keep.tile([P, D, PACK], BF16, name="vg%d" % b, align_bytes=64) for b in range(B)]
         vq = [keep.tile([P, D], U32, name="vq%d" % b, align_bytes=64) for b in range(B)]
         vs = [keep.tile([P, D], U8, name="vs%d" % b, align_bytes=64) for b in range(B)]
         og = [keep.tile([P, S, PACK], BF16, name="og%d" % b, align_bytes=64) for b in range(B)]
@@ -73,6 +74,10 @@ def tile_mixturedenserandomsynthesizer_x2_kernel(
                 c_ps[:], lhsT=ones[:], rhs=c_row[:].rearrange("p (a t c) -> p a c t", t=TILES, c=PAIR),
                 start=True, stop=True,
             )
+
+        def stage(user):
+            tl = keep.tile([P, HALF, PACK], BF16, name="stage_%s" % "_".join(map(str, SHARES.get(user, user))), align_bytes=64)
+            return tl
 
         def load_rows(dst, rows, t0, t1):
             if t1 - t0 == 1:
@@ -130,9 +135,9 @@ def tile_mixturedenserandomsynthesizer_x2_kernel(
                     nc.tensor.transpose(xt[:, i, h, :], words[:, h : 2 * P : 2], ident[:])
             state["xt", n] = xt
 
-        def x_evac(n, cnt):
-            xg = work.tile([P, 2, P, PACK], BF16, name="xg", align_bytes=64)
-            nc.scalar.copy(
+        def x_evac(n, cnt, eng="s"):
+            xg = stage(("x", n))[:].rearrange("p (i n) j -> p i n j", i=2)
+            copier(eng)(
                 out=xg[:, 0:cnt].rearrange("p i n j -> p (i n j)").bitcast(F32).rearrange("p (i n h) -> p i n h", h=2, i=cnt),
                 in_=state["xt", n][:, 0:cnt].rearrange("p i h n -> p i n h"),
             )
@@ -196,7 +201,7 @@ def tile_mixturedenserandomsynthesizer_x2_kernel(
             state["pt", n] = pt
 
         def p_evac(n, cnt):
-            pg = work.tile([P, 2, P, PACK], BF16, name="pg", align_bytes=64)
+            pg = stage(("p", n))[:].rearrange("p (i n) j -> p i n j", i=2)
             nc.scalar.copy(
                 out=pg[:, 0:cnt].rearrange("p i n j -> p (i n j)").bitcast(F32).rearrange("p (i n h) -> p i n h", h=2, i=cnt),
                 in_=state["pt", n][:, 0:cnt].rearrange("p i h n -> p i n h"),
@@ -232,23 +237,20 @@ def tile_mixturedenserandomsynthesizer_x2_kernel(
                 func=ACT.Copy, scale=u_f[:, t : t + 1],
             )
 
-        def v_pack(b, c0, c1):
-            nc.vector.tensor_copy(
-                out=vg[b][:, c0:c1, :].rearrange("p (c i) t -> p c t i", i=PACK),
-                in_=vn[b][:, :, c0:c1].rearrange("p t (c i) -> p c t i", i=PACK),
+        def v_pack(b, half):
+            cols = slice(HALF * half, HALF * (half + 1))
+            vg = stage(("v", b, half))
+            nc.gpsimd.tensor_scalar(
+                out=vg[:], in0=vn[b][:, :, cols].rearrange("p t c -> p c t"),
+                scalar1=1.0, scalar2=0.0, op0=ALU.mult, op1=ALU.add,
             )
+            state["vg", b, half] = vg
 
-        def v_pack_g(b, pieces):
-            w = D // pieces
-            for c0 in range(0, D, w):
-                nc.gpsimd.tensor_scalar(
-                    out=vg[b][:, c0 : c0 + w, :], in0=vn[b][:, :, c0 : c0 + w].rearrange("p t c -> p c t"),
-                    scalar1=1.0, scalar2=0.0, op0=ALU.mult, op1=ALU.add,
-                )
-
-        def v_quant(b):
+        def v_quant(b, half):
+            cols = slice(HALF * half, HALF * (half + 1))
             nc.vector.quantize_mx(
-                out=vq[b][:].bitcast(X4), scales=vs[b][:], in_=vg[b][:].rearrange("p n j -> p (n j)")
+                out=vq[b][:, cols].bitcast(X4), scales=vs[b][:, cols],
+                in_=state["vg", b, half][:].rearrange("p n j -> p (n j)"),
             )
 
         def nat_mm(n):
@@ -319,16 +321,16 @@ def tile_mixturedenserandomsynthesizer_x2_kernel(
         make_identity(nc, ident[:])
         load_x(0)
         load_x(1)
+        load_x(2)
         load_words(w_sb, w_words)
-        load_rnd(0)
         load_scales(ws_sb, w_scales)
         for par in range(PAIR):
             nc.gpsimd.dma_start(
                 out=u_bf[par:P:PAIR, 0:7], in_=u.rearrange("(a j) -> a j", j=8)[:, par : par + 7]
             )
+        load_rnd(0)
         load_rnd(1)
         load_words(wv_sb, wv_words)
-        load_x(2)
         load_scales(wvs_sb, wv_scales)
         load_rnd(2)
         nc.sync.dma_start(out=c_row[0:1, :], in_=c.rearrange("(o k) -> o k", o=1))
@@ -336,8 +338,10 @@ def tile_mixturedenserandomsynthesizer_x2_kernel(
 
         x_turn(0, 1)
         x_turn(1, 1)
+        x_turn(2, 2)
         x_evac(0, 1)
         x_evac(1, 1)
+        x_evac(2, 2)
         x_quant(0, 1)
         syn(0)
         x_quant(1, 1)
@@ -345,141 +349,143 @@ def tile_mixturedenserandomsynthesizer_x2_kernel(
         syn(1)
         rnd_mix(1, "v")
         nc.gpsimd.tensor_copy(out=u_f[:], in_=u_bf[:, 0:7:2])
-        x_turn(2, 2)
+        rnd_mix(2, "g")
+        rnd_mix(3, "g")
         v_mm(0)
         v_mm(1)
-        spread_c()
         logit(0)
-        logit(1)
-        x_evac(2, 2)
-        row_max(0, 1)
-        expo(0)
-        v_gain(0)
-        row_max(1, 1)
         x_quant(2, 2)
         syn(2)
-        syn(3)
         v_mm(2)
+        logit(1)
+        v_gain(0)
         v_mm(3)
+        syn(3)
+        spread_c()
+        row_max(0, 1)
+        expo(0)
         x_turn(4, 2)
+        row_max(1, 1)
+        v_gain(1)
         x_turn(6, 2)
         expo(1)
-        v_gain(1)
-        rnd_mix(2, "v")
+        logit(2)
         recip(0, 1)
-        rnd_mix(3, "v")
+        row_max(2, 1)
         pc(0)
         p_turn(0, 1)
-        v_gain(2)
-        v_gain(3)
-        v_pack_g(0, 4)
         x_evac(4, 2)
-        p_evac(0, 1)
+        v_gain(2)
         x_evac(6, 2)
-        logit(2)
-        logit(3)
+        v_gain(3)
         recip(1, 1)
-        row_max(2, 1)
+        logit(3)
         pc(1)
         p_turn(1, 1)
         x_quant(4, 2)
         syn(4)
         v_mm(4)
         v_mm(5)
-        syn(5)
-        expo(2)
-        p_evac(1, 1)
         row_max(3, 1)
-        expo(3)
         x_quant(6, 2)
+        v_pack(0, 0)
+        syn(5)
         v_mm(6)
         v_mm(7)
-        p_quant(0, 1)
+        expo(2)
+        p_evac(0, 1)
+        expo(3)
+        p_evac(1, 1)
         recip(2, 1)
         logit(4)
-        v_gain(4)
-        v_gain(5)
-        v_gain(6)
-        v_gain(7)
-        v_pack_g(1, 4)
         pc(2)
         p_turn(2, 1)
         syn(6)
         row_max(4, 1)
-        p_quant(1, 1)
-        v_quant(0)
-        nat_mm(0)
-        quad_mm(0, 0, P)
-        nat_mm(1)
+        p_quant(0, 1)
+        v_pack(0, 1)
+        v_gain(4)
+        v_gain(5)
         expo(4)
         p_evac(2, 1)
+        v_gain(6)
+        v_gain(7)
         recip(3, 1)
         logit(5)
         pc(3)
         p_turn(3, 1)
         syn(7)
-        quad_mm(1, 0, P)
         row_max(5, 1)
-        p_quant(2, 1)
-        nat_evac(0, "s")
-        quad_evac(0, 0, P, "s")
-        nat_mm(2)
+        v_quant(0, 0)
+        v_quant(0, 1)
+        p_quant(1, 1)
+        v_pack(1, 0)
+        nat_mm(0)
+        quad_mm(0, 0, P)
+        nat_mm(1)
         expo(5)
         p_evac(3, 1)
         recip(4, 1)
         logit(6)
         pc(4)
+        quad_mm(1, 0, P)
         p_turn(4, 1)
-        quad_mm(2, 0, P)
         row_max(6, 1)
+        p_quant(2, 1)
         p_quant(3, 1)
-        nat_mm(3)
-        nat_evac(1, "s")
-        quad_evac(1, 0, P, "s")
-        nat_evac(2, "s")
+        v_pack(1, 1)
+        nat_evac(0, "s")
+        nat_mm(2)
+        quad_evac(0, 0, P, "s")
+        quad_mm(2, 0, P)
         expo(6)
         p_evac(4, 1)
+        nat_evac(1, "s")
+        nat_mm(3)
         recip(5, 1)
         logit(7)
         pc(5)
         p_turn(5, 1)
-        quad_mm(3, 0, P)
         row_max(7, 1)
-        p_quant(4, 1)
-        quad_evac(2, 0, P, "s")
+        quad_evac(1, 0, P, "s")
+        quad_mm(3, 0, P)
         expo(7)
         p_evac(5, 1)
+        p_quant(4, 1)
         recip(6, 1)
-        v_quant(1)
-        nat_mm(4)
+        v_quant(1, 0)
+        v_quant(1, 1)
         pc(6)
         p_turn(6, 1)
-        quad_mm(4, 0, P)
         recip(7, 1)
         p_quant(5, 1)
-        nat_evac(3, "s")
-        quad_evac(3, 0, P, "s")
+        nat_evac(2, "s")
+        nat_mm(4)
+        quad_evac(2, 0, P, "s")
+        quad_mm(4, 0, P)
         pc(7)
         p_turn(7, 1)
-        nat_mm(5)
-        quad_mm(5, 0, P)
         p_evac(6, 1)
+        quad_evac(3, 0, P, "v")
+        nat_mm(5)
+        p_quant(6, 1)
+        nat_evac(3, "s")
+        quad_mm(5, 0, P)
+        p_evac(7, 1)
         o_quant(0, 0, S)
         o_scales(0, [nc.sync] * 4)
+        p_quant(7, 1)
         nat_evac(4, "s")
-        p_evac(7, 1)
-        p_quant(6, 1)
-        nat_mm(6)
         quad_mm(6, 0, P)
         quad_evac(4, 0, P, "v")
-        p_quant(7, 1)
         quad_mm(7, 0, P)
-        nat_mm(7)
         nat_evac(5, "s")
+        nat_mm(6)
         quad_evac(5, 0, P, "v")
-        nat_evac(6, "s")
+        nat_mm(7)
         quad_evac(6, 0, P, "s")
         quad_evac(7, 0, P, "v")
-        nat_evac(7, "s")
+        nat_evac(6, "s")
         o_quant(1, 0, S)
-        o_scales(1, [nc.sync, nc.scalar, nc.sync, nc.scalar])
+        nat_evac(7, "s")
+        o_scales(1, [nc.sync] * 4)

@@ -21,8 +21,7 @@ PACK = 4
 TILES = S // P
 N_TILES = B * TILES
 PAIR = 2
-HALF = D // 2
-SHARES = {("v", 0, 0): ("x", 6), ("v", 0, 1): ("p", 0), ("v", 1, 0): ("p", 1), ("v", 1, 1): ("p", 3)}
+SHARES = {("v", 0): ("x", 6), ("v", 1): ("p", 0)}
 
 
 def tile_mixturedenserandomsynthesizer_x2_kernel(
@@ -59,7 +58,7 @@ def tile_mixturedenserandomsynthesizer_x2_kernel(
         vs = [keep.tile([P, D], U8, name="vs%d" % b, align_bytes=64) for b in range(B)]
         og = [keep.tile([P, S, PACK], BF16, name="og%d" % b, align_bytes=64) for b in range(B)]
         oq = [keep.tile([P, S], U32, name="oq%d" % b, align_bytes=64) for b in range(B)]
-        os_ = [keep.tile([P, S], U8, name="os%d" % b, align_bytes=64) for b in range(B)]
+        os_ = keep.tile([P, B * S], U8, name="os_", align_bytes=64)
         pq = keep.tile([P, N_TILES * P], U32, name="pq", align_bytes=64)
         pqs = keep.tile([P, N_TILES * P], U8, name="pqs", align_bytes=64)
         lg = keep.tile([P, N_TILES, S], F32, name="lg")
@@ -76,7 +75,7 @@ def tile_mixturedenserandomsynthesizer_x2_kernel(
             )
 
         def stage(user):
-            tl = keep.tile([P, HALF, PACK], BF16, name="stage_%s" % "_".join(map(str, SHARES.get(user, user))), align_bytes=64)
+            tl = keep.tile([P, D, PACK], BF16, name="stage_%s" % "_".join(map(str, SHARES.get(user, user))), align_bytes=64)
             return tl
 
         def load_rows(dst, rows, t0, t1):
@@ -136,7 +135,7 @@ def tile_mixturedenserandomsynthesizer_x2_kernel(
             state["xt", n] = xt
 
         def x_evac(n, cnt, eng="s"):
-            xg = stage(("x", n))[:].rearrange("p (i n) j -> p i n j", i=2)
+            xg = stage(("x", n))[:, 0 : 2 * P].rearrange("p (i n) j -> p i n j", i=2)
             copier(eng)(
                 out=xg[:, 0:cnt].rearrange("p i n j -> p (i n j)").bitcast(F32).rearrange("p (i n h) -> p i n h", h=2, i=cnt),
                 in_=state["xt", n][:, 0:cnt].rearrange("p i h n -> p i n h"),
@@ -192,16 +191,15 @@ def tile_mixturedenserandomsynthesizer_x2_kernel(
             )
             state["pcs", n] = pcs
 
-        def p_turn(n, cnt):
-            pt = acc_bank()[:].rearrange("p (i h n) -> p i h n", i=2, h=2)
-            for i in range(cnt):
-                words = state["pcs", n + i][:].bitcast(F32)
-                for h in range(2):
-                    nc.tensor.transpose(pt[:, i, h, :], words[:, h : 2 * P : 2], ident[:])
-            state["pt", n] = pt
+        def p_turn(n, i=0):
+            if i == 0:
+                state["pt", n] = acc_bank()[:].rearrange("p (i h n) -> p i h n", i=2, h=2)
+            words = state["pcs", n][:].bitcast(F32)
+            for h in range(2):
+                nc.tensor.transpose(state["pt", n - i][:, i, h, :], words[:, h : 2 * P : 2], ident[:])
 
         def p_evac(n, cnt):
-            pg = stage(("p", n))[:].rearrange("p (i n) j -> p i n j", i=2)
+            pg = stage(("p", n))[:, 0 : 2 * P].rearrange("p (i n) j -> p i n j", i=2)
             nc.scalar.copy(
                 out=pg[:, 0:cnt].rearrange("p i n j -> p (i n j)").bitcast(F32).rearrange("p (i n h) -> p i n h", h=2, i=cnt),
                 in_=state["pt", n][:, 0:cnt].rearrange("p i h n -> p i n h"),
@@ -237,20 +235,17 @@ def tile_mixturedenserandomsynthesizer_x2_kernel(
                 func=ACT.Copy, scale=u_f[:, t : t + 1],
             )
 
-        def v_pack(b, half):
-            cols = slice(HALF * half, HALF * (half + 1))
-            vg = stage(("v", b, half))
+        def v_pack(b):
+            vg = stage(("v", b))
             nc.gpsimd.tensor_scalar(
-                out=vg[:], in0=vn[b][:, :, cols].rearrange("p t c -> p c t"),
+                out=vg[:], in0=vn[b][:].rearrange("p t c -> p c t"),
                 scalar1=1.0, scalar2=0.0, op0=ALU.mult, op1=ALU.add,
             )
-            state["vg", b, half] = vg
+            state["vg", b] = vg
 
-        def v_quant(b, half):
-            cols = slice(HALF * half, HALF * (half + 1))
+        def v_quant(b):
             nc.vector.quantize_mx(
-                out=vq[b][:, cols].bitcast(X4), scales=vs[b][:, cols],
-                in_=state["vg", b, half][:].rearrange("p n j -> p (n j)"),
+                out=vq[b][:].bitcast(X4), scales=vs[b][:], in_=state["vg", b][:].rearrange("p n j -> p (n j)")
             )
 
         def nat_mm(n):
@@ -298,7 +293,7 @@ def tile_mixturedenserandomsynthesizer_x2_kernel(
 
         def o_quant(b, i0, i1):
             nc.vector.quantize_mx(
-                out=oq[b][:, i0:i1].bitcast(X4), scales=os_[b][:, i0:i1],
+                out=oq[b][:, i0:i1].bitcast(X4), scales=os_[:, S * b + i0 : S * b + i1],
                 in_=og[b][:, i0:i1, :].rearrange("m i d -> m (i d)"),
             )
             nc.sync.dma_start(
@@ -306,11 +301,10 @@ def tile_mixturedenserandomsynthesizer_x2_kernel(
                 in_=oq[b][:, i0:i1].bitcast(I32),
             )
 
-        def o_scales(b, queues):
+        def o_scales():
             for q in range(4):
-                queues[q].dma_start(
-                    out=out_2[0, 4 * q : 4 * q + 4, S * b : S * (b + 1)].bitcast(I32),
-                    in_=os_[b][32 * q : 32 * q + 4, :].bitcast(I32),
+                nc.sync.dma_start(
+                    out=out_2[0, 4 * q : 4 * q + 4, :].bitcast(I32), in_=os_[32 * q : 32 * q + 4, :].bitcast(I32)
                 )
 
         nc.vector.memset(ws_sb[:].bitcast(I32), 0)
@@ -333,8 +327,6 @@ def tile_mixturedenserandomsynthesizer_x2_kernel(
         load_words(wv_sb, wv_words)
         load_scales(wvs_sb, wv_scales)
         load_rnd(2)
-        nc.sync.dma_start(out=c_row[0:1, :], in_=c.rearrange("(o k) -> o k", o=1))
-        load_x(3)
 
         x_turn(0, 1)
         x_turn(1, 1)
@@ -345,6 +337,8 @@ def tile_mixturedenserandomsynthesizer_x2_kernel(
         x_quant(0, 1)
         syn(0)
         x_quant(1, 1)
+        nc.sync.dma_start(out=c_row[0:1, :], in_=c.rearrange("(o k) -> o k", o=1))
+        load_x(3)
         rnd_mix(0, "v")
         syn(1)
         rnd_mix(1, "v")
@@ -373,98 +367,88 @@ def tile_mixturedenserandomsynthesizer_x2_kernel(
         recip(0, 1)
         row_max(2, 1)
         pc(0)
-        p_turn(0, 1)
+        p_turn(0)
         x_evac(4, 2)
-        v_gain(2)
         x_evac(6, 2)
+        v_gain(2)
         v_gain(3)
         recip(1, 1)
         logit(3)
-        pc(1)
-        p_turn(1, 1)
         x_quant(4, 2)
         syn(4)
         v_mm(4)
+        pc(1)
+        p_turn(1, 1)
         v_mm(5)
-        row_max(3, 1)
         x_quant(6, 2)
-        v_pack(0, 0)
+        v_pack(0)
+        row_max(3, 1)
         syn(5)
         v_mm(6)
         v_mm(7)
         expo(2)
-        p_evac(0, 1)
         expo(3)
-        p_evac(1, 1)
-        recip(2, 1)
+        p_evac(0, 2)
         logit(4)
-        pc(2)
-        p_turn(2, 1)
-        syn(6)
+        recip(2, 1)
         row_max(4, 1)
-        p_quant(0, 1)
-        v_pack(0, 1)
+        pc(2)
+        syn(6)
+        p_turn(2)
         v_gain(4)
         v_gain(5)
         expo(4)
-        p_evac(2, 1)
         v_gain(6)
         v_gain(7)
         recip(3, 1)
         logit(5)
         pc(3)
-        p_turn(3, 1)
         syn(7)
+        p_turn(3, 1)
         row_max(5, 1)
-        v_quant(0, 0)
-        v_quant(0, 1)
-        p_quant(1, 1)
-        v_pack(1, 0)
+        v_quant(0)
+        p_quant(0, 2)
+        v_pack(1)
         nat_mm(0)
         quad_mm(0, 0, P)
-        nat_mm(1)
         expo(5)
-        p_evac(3, 1)
+        p_evac(2, 2)
         recip(4, 1)
         logit(6)
         pc(4)
+        nat_mm(1)
+        p_turn(4)
         quad_mm(1, 0, P)
-        p_turn(4, 1)
         row_max(6, 1)
-        p_quant(2, 1)
-        p_quant(3, 1)
-        v_pack(1, 1)
         nat_evac(0, "s")
-        nat_mm(2)
         quad_evac(0, 0, P, "s")
-        quad_mm(2, 0, P)
         expo(6)
-        p_evac(4, 1)
         nat_evac(1, "s")
-        nat_mm(3)
         recip(5, 1)
         logit(7)
         pc(5)
         p_turn(5, 1)
         row_max(7, 1)
         quad_evac(1, 0, P, "s")
-        quad_mm(3, 0, P)
         expo(7)
-        p_evac(5, 1)
-        p_quant(4, 1)
+        p_evac(4, 2)
+        p_quant(2, 2)
+        nat_mm(2)
+        quad_mm(2, 0, P)
+        quad_mm(3, 0, P)
         recip(6, 1)
-        v_quant(1, 0)
-        v_quant(1, 1)
+        v_quant(1)
         pc(6)
-        p_turn(6, 1)
+        p_turn(6)
+        nat_mm(3)
         recip(7, 1)
-        p_quant(5, 1)
+        p_quant(4, 2)
         nat_evac(2, "s")
-        nat_mm(4)
         quad_evac(2, 0, P, "s")
-        quad_mm(4, 0, P)
         pc(7)
-        p_turn(7, 1)
+        nat_mm(4)
+        p_turn(7)
+        quad_mm(4, 0, P)
         p_evac(6, 1)
         quad_evac(3, 0, P, "v")
         nat_mm(5)
@@ -473,19 +457,18 @@ def tile_mixturedenserandomsynthesizer_x2_kernel(
         quad_mm(5, 0, P)
         p_evac(7, 1)
         o_quant(0, 0, S)
-        o_scales(0, [nc.sync] * 4)
+        nat_mm(6)
         p_quant(7, 1)
         nat_evac(4, "s")
-        quad_mm(6, 0, P)
-        quad_evac(4, 0, P, "v")
         quad_mm(7, 0, P)
+        quad_evac(4, 0, P, "v")
+        quad_mm(6, 0, P)
         nat_evac(5, "s")
-        nat_mm(6)
-        quad_evac(5, 0, P, "v")
         nat_mm(7)
-        quad_evac(6, 0, P, "s")
-        quad_evac(7, 0, P, "v")
+        quad_evac(5, 0, P, "v")
         nat_evac(6, "s")
-        o_quant(1, 0, S)
+        quad_evac(7, 0, P, "v")
+        quad_evac(6, 0, P, "s")
         nat_evac(7, "s")
-        o_scales(1, [nc.sync] * 4)
+        o_quant(1, 0, S)
+        o_scales()

@@ -44,7 +44,7 @@ def tile_mixturedenserandomsynthesizer_x2_kernel(
         wvs_sb = keep.tile([P, D], U8, name="wvs_sb", align_bytes=64)
         rm = keep.tile([P, TILES, S], F32, name="rm")
         mix_bf = keep.tile([P, 2], BF16, name="mix_bf")
-        u_bf = keep.tile([P, 8], BF16, name="u_bf")
+        u_bf = keep.tile([P, TILES], BF16, name="u_bf")
         u_f = keep.tile([P, TILES], F32, name="u_f")
         c_row = keep.tile([P, S], BF16, name="c_row")
         ones = keep.tile([P, P], BF16, name="ones")
@@ -70,7 +70,7 @@ def tile_mixturedenserandomsynthesizer_x2_kernel(
 
         def spread_c():
             nc.tensor.matmul(
-                c_ps[:], lhsT=ones[:], rhs=c_row[:].rearrange("p (a t c) -> p a c t", t=TILES, c=PAIR),
+                c_ps[:], lhsT=ones[:], rhs=c_row[:],
                 start=True, stop=True,
             )
 
@@ -79,16 +79,7 @@ def tile_mixturedenserandomsynthesizer_x2_kernel(
             return tl
 
         def load_rows(dst, rows, t0, t1):
-            if t1 - t0 == 1:
-                nc.sync.dma_start(
-                    out=dst[:, 0, :], in_=rows.rearrange("(a t c) f -> t a c f", t=TILES, c=PAIR)[t0]
-                )
-            else:
-                for par in range(PAIR):
-                    nc.sync.dma_start(
-                        out=dst[par:P:PAIR, :, :],
-                        in_=rows.rearrange("(a t c) f -> c a t f", t=TILES, c=PAIR)[par, :, t0:t1, :],
-                    )
+            nc.sync.dma_start(out=dst[:], in_=rows.rearrange("(p t) f -> p t f", t=TILES)[:, t0:t1, :])
 
         def load_x(g):
             n0, n1 = x_groups[g]
@@ -174,8 +165,7 @@ def tile_mixturedenserandomsynthesizer_x2_kernel(
         def expo(n):
             e = work.tile([P, S], F32, name="e")
             nc.scalar.activation(
-                out=e[:].rearrange("p (a c t) -> p a c t", t=TILES, c=PAIR),
-                in_=lg[:, n, :].rearrange("p (a t c) -> p a c t", t=TILES, c=PAIR),
+                out=e[:], in_=lg[:, n, :],
                 func=ACT.Exp, bias=nmax[:, n : n + 1], scale=1.0, accum_out=tot[:, n : n + 1],
             )
             state["e", n] = e
@@ -199,18 +189,20 @@ def tile_mixturedenserandomsynthesizer_x2_kernel(
                 nc.tensor.transpose(state["pt", n - i][:, i, h, :], words[:, h : 2 * P : 2], ident[:])
 
         def p_evac(n, cnt):
-            pg = stage(("p", n))[:, 0 : 2 * P].rearrange("p (i n) j -> p i n j", i=2)
+            pg = stage(("p", n))[:, 0 : cnt * P].rearrange("p n j -> p (n j)")
             nc.scalar.copy(
-                out=pg[:, 0:cnt].rearrange("p i n j -> p (i n j)").bitcast(F32).rearrange("p (i n h) -> p i n h", h=2, i=cnt),
-                in_=state["pt", n][:, 0:cnt].rearrange("p i h n -> p i n h"),
+                out=pg.bitcast(F32).rearrange("p (n i h) -> p n i h", h=2, i=cnt),
+                in_=state["pt", n][:, 0:cnt].rearrange("p i h n -> p n i h"),
             )
             state["pg", n] = pg
+            for i in range(cnt):
+                state["rows", n + i] = (slice(P // cnt * i, P // cnt * (i + 1)), slice(n % TILES, n % TILES + cnt))
 
         def p_quant(n, cnt):
             cols = slice(P * n, P * (n + cnt))
             nc.vector.quantize_mx(
                 out=pq[:, cols].bitcast(X4), scales=pqs[:, cols],
-                in_=state["pg", n][:, 0:cnt].rearrange("p i n j -> p (i n j)"),
+                in_=state["pg", n],
             )
 
         def acc_bank():
@@ -279,16 +271,14 @@ def tile_mixturedenserandomsynthesizer_x2_kernel(
                 out=ob[:].rearrange("p (m d) -> p m d", d=PACK),
                 in_=state["nat", n][:].rearrange("p (d m) -> p m d", d=PACK),
             )
-            nc.sync.dma_start(
-                out=out_0[b].rearrange("(a t c) d -> t a c d", t=TILES, c=PAIR)[t], in_=ob[:]
-            )
+            ps, ts = state["rows", n]
+            nc.sync.dma_start(out=out_0[b].rearrange("(p t) d -> p t d", t=TILES)[ps, ts, :], in_=ob[:])
 
         def quad_evac(n, p0, p1, eng):
-            b, t = divmod(n, TILES)
-            w = p1 - p0
+            ps, ts = state["rows", n]
             copier(eng)(
-                out=og[b][:].rearrange("m (a t c) d -> m t a c d", t=TILES, c=PAIR)[:, t, p0 // PAIR : p1 // PAIR],
-                in_=state["qd", n, p0][:, 0 : PACK * w].rearrange("m (d a c) -> m a c d", d=PACK, c=PAIR),
+                out=og[n // TILES][:].rearrange("m (p t) d -> m p t d", t=TILES)[:, ps, ts, :],
+                in_=state["qd", n, p0][:].rearrange("m (d p i) -> m p i d", d=PACK, i=ts.stop - ts.start),
             )
 
         def o_quant(b, i0, i1):
@@ -318,10 +308,7 @@ def tile_mixturedenserandomsynthesizer_x2_kernel(
         load_x(2)
         load_words(w_sb, w_words)
         load_scales(ws_sb, w_scales)
-        for par in range(PAIR):
-            nc.gpsimd.dma_start(
-                out=u_bf[par:P:PAIR, 0:7], in_=u.rearrange("(a j) -> a j", j=8)[:, par : par + 7]
-            )
+        nc.gpsimd.dma_start(out=u_bf[:], in_=u.rearrange("(p t) -> p t", t=TILES))
         load_rnd(0)
         load_rnd(1)
         load_words(wv_sb, wv_words)
@@ -342,7 +329,7 @@ def tile_mixturedenserandomsynthesizer_x2_kernel(
         rnd_mix(0, "v")
         syn(1)
         rnd_mix(1, "v")
-        nc.gpsimd.tensor_copy(out=u_f[:], in_=u_bf[:, 0:7:2])
+        nc.gpsimd.tensor_copy(out=u_f[:], in_=u_bf[:])
         rnd_mix(2, "g")
         rnd_mix(3, "g")
         v_mm(0)

@@ -261,6 +261,26 @@ def tile_mixturedenserandomsynthesizer_x2_kernel(
                 )
             state["qd", n, p0] = qd
 
+        def quad_mm_last(i, half):
+            if i == 0:
+                state["qd", 6 + half, 0] = acc_bank()
+            qd = state["qd", 6 + half, 0][:].rearrange("m (d i p) -> m d i p", d=PACK, i=PAIR)
+            w = P // PAIR
+            cols = slice(P * (6 + i) + w * half, P * (6 + i) + w * (half + 1))
+            for d in range(PACK):
+                fcols = slice(P * d, P * (d + 1))
+                nc.tensor.matmul_mx(
+                    out=qd[:, d, i, :], lhsT=vq[1][:, fcols].bitcast(X4), lhsT_scale=vs[1][:, fcols],
+                    rhs=pq[:, cols].bitcast(X4), rhs_scale=pqs[:, cols], start=True, stop=True,
+                )
+
+        def quad_evac_last(half, eng):
+            w = P // PAIR
+            copier(eng)(
+                out=og[1][:].rearrange("m (p t) d -> m p t d", t=TILES)[:, w * half : w * (half + 1), 2:4, :],
+                in_=state["qd", 6 + half, 0][:].rearrange("m (d i p) -> m p i d", d=PACK, i=PAIR),
+            )
+
         def copier(eng):
             return nc.scalar.copy if eng == "s" else nc.vector.tensor_copy
 
@@ -300,20 +320,22 @@ def tile_mixturedenserandomsynthesizer_x2_kernel(
         nc.vector.memset(ws_sb[:].bitcast(I32), 0)
         nc.vector.memset(c_row[:], 0.0)
         nc.vector.memset(wvs_sb[:].bitcast(I32), 0)
-        nc.scalar.activation(out=ones[:], in_=c_row[:, 0:P], func=ACT.Copy, bias=1.0)
         nc.gpsimd.dma_start(out=mix_bf[:], in_=mix.partition_broadcast(P))
         make_identity(nc, ident[:])
+        nc.scalar.activation(out=ones[:], in_=c_row[:, 0:P], func=ACT.Copy, bias=1.0)
         load_x(0)
         load_x(1)
         load_x(2)
-        load_words(w_sb, w_words)
         load_scales(ws_sb, w_scales)
+        load_words(w_sb, w_words)
         nc.gpsimd.dma_start(out=u_bf[:], in_=u.rearrange("(p t) -> p t", t=TILES))
         load_rnd(0)
         load_rnd(1)
         load_words(wv_sb, wv_words)
         load_scales(wvs_sb, wv_scales)
         load_rnd(2)
+        nc.sync.dma_start(out=c_row[0:1, :], in_=c.rearrange("(o k) -> o k", o=1))
+        load_x(3)
 
         x_turn(0, 1)
         x_turn(1, 1)
@@ -324,12 +346,10 @@ def tile_mixturedenserandomsynthesizer_x2_kernel(
         x_quant(0, 1)
         syn(0)
         x_quant(1, 1)
-        nc.sync.dma_start(out=c_row[0:1, :], in_=c.rearrange("(o k) -> o k", o=1))
-        load_x(3)
         rnd_mix(0, "v")
         syn(1)
         rnd_mix(1, "v")
-        nc.gpsimd.tensor_copy(out=u_f[:], in_=u_bf[:])
+        nc.scalar.copy(out=u_f[:], in_=u_bf[:])
         rnd_mix(2, "g")
         rnd_mix(3, "g")
         v_mm(0)
@@ -344,63 +364,61 @@ def tile_mixturedenserandomsynthesizer_x2_kernel(
         syn(3)
         spread_c()
         row_max(0, 1)
+        v_gain(1)
         expo(0)
         x_turn(4, 2)
         row_max(1, 1)
-        v_gain(1)
+        v_gain(2)
         x_turn(6, 2)
         expo(1)
         logit(2)
-        recip(0, 1)
+        logit(3)
         row_max(2, 1)
-        pc(0)
-        p_turn(0)
+        recip(0, 2)
+        row_max(3, 1)
         x_evac(4, 2)
         x_evac(6, 2)
-        v_gain(2)
         v_gain(3)
-        recip(1, 1)
-        logit(3)
         x_quant(4, 2)
         syn(4)
         v_mm(4)
-        pc(1)
-        p_turn(1, 1)
+        syn(5)
+        pc(0)
+        p_turn(0)
         v_mm(5)
         x_quant(6, 2)
         v_pack(0)
-        row_max(3, 1)
-        syn(5)
+        pc(1)
+        p_turn(1, 1)
         v_mm(6)
         v_mm(7)
         expo(2)
         expo(3)
-        p_evac(0, 2)
-        logit(4)
-        recip(2, 1)
-        row_max(4, 1)
-        pc(2)
-        syn(6)
-        p_turn(2)
         v_gain(4)
         v_gain(5)
-        expo(4)
-        v_gain(6)
-        v_gain(7)
-        recip(3, 1)
+        p_evac(0, 2)
+        logit(4)
+        syn(6)
         logit(5)
-        pc(3)
         syn(7)
-        p_turn(3, 1)
+        row_max(4, 1)
+        recip(2, 2)
         row_max(5, 1)
+        pc(2)
+        p_turn(2)
+        pc(3)
+        p_turn(3, 1)
+        v_gain(6)
+        expo(4)
+        expo(5)
+        v_gain(7)
         v_quant(0)
         p_quant(0, 2)
         v_pack(1)
         nat_mm(0)
         quad_mm(0, 0, P)
-        expo(5)
         p_evac(2, 2)
-        recip(4, 1)
+        recip(4, 2)
         logit(6)
         pc(4)
         nat_mm(1)
@@ -409,9 +427,8 @@ def tile_mixturedenserandomsynthesizer_x2_kernel(
         row_max(6, 1)
         nat_evac(0, "s")
         quad_evac(0, 0, P, "s")
-        expo(6)
         nat_evac(1, "s")
-        recip(5, 1)
+        expo(6)
         logit(7)
         pc(5)
         p_turn(5, 1)
@@ -445,17 +462,20 @@ def tile_mixturedenserandomsynthesizer_x2_kernel(
         p_evac(7, 1)
         o_quant(0, 0, S)
         nat_mm(6)
+        quad_mm_last(0, 0)
+        quad_mm_last(0, 1)
         p_quant(7, 1)
         nat_evac(4, "s")
-        quad_mm(7, 0, P)
+        quad_mm_last(1, 0)
+        quad_mm_last(1, 1)
         quad_evac(4, 0, P, "v")
-        quad_mm(6, 0, P)
-        nat_evac(5, "s")
         nat_mm(7)
+        nat_evac(5, "s")
         quad_evac(5, 0, P, "v")
         nat_evac(6, "s")
-        quad_evac(7, 0, P, "v")
-        quad_evac(6, 0, P, "s")
+        quad_evac_last(0, "v")
+        quad_evac_last(1, "s")
+        o_quant(1, 0, S // 2)
+        o_quant(1, S // 2, S)
         nat_evac(7, "s")
-        o_quant(1, 0, S)
         o_scales()

@@ -70,7 +70,7 @@ def tile_mixturedenserandomsynthesizer_x2_kernel(
 
         def spread_c():
             nc.tensor.matmul(
-                c_ps[:], lhsT=ones[:], rhs=c_row[:],
+                c_ps[:], lhsT=ones[:], rhs=c_row[:].rearrange("p (m h j) -> p h m j", h=2, j=2),
                 start=True, stop=True,
             )
 
@@ -165,7 +165,8 @@ def tile_mixturedenserandomsynthesizer_x2_kernel(
         def expo(n):
             e = work.tile([P, S], F32, name="e")
             nc.scalar.activation(
-                out=e[:], in_=lg[:, n, :],
+                out=e[:].rearrange("p (h m j) -> p h m j", h=2, j=2),
+                in_=lg[:, n, :].rearrange("p (m h j) -> p h m j", h=2, j=2),
                 func=ACT.Exp, bias=nmax[:, n : n + 1], scale=1.0, accum_out=tot[:, n : n + 1],
             )
             state["e", n] = e
@@ -186,7 +187,7 @@ def tile_mixturedenserandomsynthesizer_x2_kernel(
                 state["pt", n] = acc_bank()[:].rearrange("p (i h n) -> p i h n", i=2, h=2)
             words = state["pcs", n][:].bitcast(F32)
             for h in range(2):
-                nc.tensor.transpose(state["pt", n - i][:, i, h, :], words[:, h : 2 * P : 2], ident[:])
+                nc.tensor.transpose(state["pt", n - i][:, i, h, :], words[:, P * h : P * (h + 1)], ident[:])
 
         def p_evac(n, cnt):
             pg = stage(("p", n))[:, 0 : cnt * P].rearrange("p n j -> p (n j)")
@@ -404,78 +405,73 @@ def tile_mixturedenserandomsynthesizer_x2_kernel(
         row_max(4, 1)
         recip(2, 2)
         row_max(5, 1)
+        v_quant(0)
+        p_quant(0, 2)
+        v_gain(6)
+        v_gain(7)
+        v_pack(1)
+        nat_mm(0)
+        quad_mm(0, 0, P)
         pc(2)
         p_turn(2)
         pc(3)
         p_turn(3, 1)
-        v_gain(6)
+        nat_mm(1)
+        quad_mm(1, 0, P)
         expo(4)
         expo(5)
-        v_gain(7)
-        v_quant(0)
-        p_quant(0, 2)
-        v_pack(1)
-        nat_mm(0)
-        quad_mm(0, 0, P)
-        p_evac(2, 2)
-        recip(4, 2)
-        logit(6)
-        pc(4)
-        nat_mm(1)
-        p_turn(4)
-        quad_mm(1, 0, P)
-        row_max(6, 1)
         nat_evac(0, "s")
-        quad_evac(0, 0, P, "s")
-        nat_evac(1, "s")
-        expo(6)
+        p_evac(2, 2)
+        logit(6)
+        recip(4, 2)
         logit(7)
-        pc(5)
-        p_turn(5, 1)
-        row_max(7, 1)
-        quad_evac(1, 0, P, "s")
-        expo(7)
-        p_evac(4, 2)
+        pc(4)
+        p_turn(4)
+        row_max(6, 1)
         p_quant(2, 2)
         nat_mm(2)
         quad_mm(2, 0, P)
+        row_max(7, 1)
+        pc(5)
+        p_turn(5, 1)
+        nat_mm(3)
         quad_mm(3, 0, P)
-        recip(6, 1)
+        quad_evac(0, 0, P, "s")
+        nat_evac(1, "s")
+        quad_evac(1, 0, P, "s")
+        expo(6)
+        expo(7)
         v_quant(1)
+        nat_evac(2, "s")
+        p_evac(4, 2)
+        recip(6, 2)
         pc(6)
         p_turn(6)
-        nat_mm(3)
-        recip(7, 1)
-        p_quant(4, 2)
-        nat_evac(2, "s")
-        quad_evac(2, 0, P, "s")
         pc(7)
+        p_turn(7, 1)
+        p_quant(4, 2)
         nat_mm(4)
-        p_turn(7)
-        quad_mm(4, 0, P)
-        p_evac(6, 1)
-        quad_evac(3, 0, P, "v")
+        quad_evac(2, 0, P, "s")
         nat_mm(5)
-        p_quant(6, 1)
-        nat_evac(3, "s")
+        quad_evac(3, 0, P, "s")
+        quad_mm(4, 0, P)
         quad_mm(5, 0, P)
-        p_evac(7, 1)
+        p_evac(6, 2)
+        nat_evac(3, "v")
         o_quant(0, 0, S)
-        nat_mm(6)
-        quad_mm_last(0, 0)
-        quad_mm_last(0, 1)
-        p_quant(7, 1)
+        p_quant(6, 2)
         nat_evac(4, "s")
-        quad_mm_last(1, 0)
-        quad_mm_last(1, 1)
-        quad_evac(4, 0, P, "v")
-        nat_mm(7)
+        nat_mm(6)
+        quad_mm(6, 0, P)
         nat_evac(5, "s")
+        nat_mm(7)
+        quad_evac(4, 0, P, "v")
+        quad_mm(7, 0, P)
         quad_evac(5, 0, P, "v")
         nat_evac(6, "s")
-        quad_evac_last(0, "v")
-        quad_evac_last(1, "s")
+        nat_evac(7, "s")
+        quad_evac(6, 0, P, "v")
+        quad_evac(7, 0, P, "s")
         o_quant(1, 0, S // 2)
         o_quant(1, S // 2, S)
-        nat_evac(7, "s")
         o_scales()

@@ -70,7 +70,7 @@ def tile_mixturedenserandomsynthesizer_x2_kernel(
 
         def spread_c():
             nc.tensor.matmul(
-                c_ps[:], lhsT=ones[:], rhs=c_row[:].rearrange("p (m h j) -> p h m j", h=2, j=2),
+                c_ps[:], lhsT=ones[:], rhs=c_row[:],
                 start=True, stop=True,
             )
 
@@ -165,8 +165,7 @@ def tile_mixturedenserandomsynthesizer_x2_kernel(
         def expo(n):
             e = work.tile([P, S], F32, name="e")
             nc.scalar.activation(
-                out=e[:].rearrange("p (h m j) -> p h m j", h=2, j=2),
-                in_=lg[:, n, :].rearrange("p (m h j) -> p h m j", h=2, j=2),
+                out=e[:], in_=lg[:, n, :],
                 func=ACT.Exp, bias=nmax[:, n : n + 1], scale=1.0, accum_out=tot[:, n : n + 1],
             )
             state["e", n] = e
@@ -187,7 +186,7 @@ def tile_mixturedenserandomsynthesizer_x2_kernel(
                 state["pt", n] = acc_bank()[:].rearrange("p (i h n) -> p i h n", i=2, h=2)
             words = state["pcs", n][:].bitcast(F32)
             for h in range(2):
-                nc.tensor.transpose(state["pt", n - i][:, i, h, :], words[:, P * h : P * (h + 1)], ident[:])
+                nc.tensor.transpose(state["pt", n - i][:, i, h, :], words[:, h : 2 * P : 2], ident[:])
 
         def p_evac(n, cnt):
             pg = stage(("p", n))[:, 0 : cnt * P].rearrange("p n j -> p (n j)")
@@ -209,6 +208,11 @@ def tile_mixturedenserandomsynthesizer_x2_kernel(
         def acc_bank():
             acc = psum.tile([P, D], F32, name="acc", bufs=7)
             return acc
+
+        def warm_up(cnt):
+            junk = acc_bank()
+            for i in range(cnt):
+                nc.tensor.matmul(junk[:], lhsT=c_row[:, 0:P], rhs=c_row[:], start=True, stop=True)
 
         def v_mm(n):
             b, t = divmod(n, TILES)
@@ -381,14 +385,15 @@ def tile_mixturedenserandomsynthesizer_x2_kernel(
         x_evac(6, 2)
         v_gain(3)
         x_quant(4, 2)
+        warm_up(2)
         syn(4)
         v_mm(4)
         syn(5)
-        pc(0)
-        p_turn(0)
-        v_mm(5)
         x_quant(6, 2)
         v_pack(0)
+        pc(0)
+        v_mm(5)
+        p_turn(0)
         pc(1)
         p_turn(1, 1)
         v_mm(6)
@@ -410,6 +415,7 @@ def tile_mixturedenserandomsynthesizer_x2_kernel(
         v_gain(6)
         v_gain(7)
         v_pack(1)
+        warm_up(2)
         nat_mm(0)
         quad_mm(0, 0, P)
         pc(2)
@@ -421,6 +427,7 @@ def tile_mixturedenserandomsynthesizer_x2_kernel(
         expo(4)
         expo(5)
         nat_evac(0, "s")
+        quad_evac(0, 0, P, "s")
         p_evac(2, 2)
         logit(6)
         recip(4, 2)
@@ -429,6 +436,7 @@ def tile_mixturedenserandomsynthesizer_x2_kernel(
         p_turn(4)
         row_max(6, 1)
         p_quant(2, 2)
+        warm_up(1)
         nat_mm(2)
         quad_mm(2, 0, P)
         row_max(7, 1)
@@ -436,16 +444,16 @@ def tile_mixturedenserandomsynthesizer_x2_kernel(
         p_turn(5, 1)
         nat_mm(3)
         quad_mm(3, 0, P)
-        quad_evac(0, 0, P, "s")
         nat_evac(1, "s")
-        quad_evac(1, 0, P, "s")
         expo(6)
+        quad_evac(1, 0, P, "s")
         expo(7)
         v_quant(1)
         nat_evac(2, "s")
         p_evac(4, 2)
         recip(6, 2)
         pc(6)
+        warm_up(1)
         p_turn(6)
         pc(7)
         p_turn(7, 1)
@@ -471,7 +479,7 @@ def tile_mixturedenserandomsynthesizer_x2_kernel(
         nat_evac(6, "s")
         nat_evac(7, "s")
         quad_evac(6, 0, P, "v")
-        quad_evac(7, 0, P, "s")
+        quad_evac(7, 0, P, "v")
         o_quant(1, 0, S // 2)
         o_quant(1, S // 2, S)
         o_scales()

@@ -21,7 +21,13 @@ PACK = 4
 TILES = S // P
 N_TILES = B * TILES
 PAIR = 2
-SHARES = {("v", 0): ("x", 6), ("v", 1): ("p", 0)}
+HALF = S // 2
+QUADRANT, SCALE_ROWS = 32, 4
+MX_ALIGN = 64
+ROTATING_BANKS = 7
+WARM_UPS = 2
+X_LOADS = ((0, 1), (1, 2), (2, 4), (4, 8))
+RND_LOADS = ((0, 1), (1, 2), (2, 4))
 
 
 def tile_mixturedenserandomsynthesizer_x2_kernel(
@@ -31,296 +37,237 @@ def tile_mixturedenserandomsynthesizer_x2_kernel(
     with ExitStack() as ctx:
         keep = ctx.enter_context(tc.tile_pool(name="keep", bufs=1))
         work = ctx.enter_context(tc.tile_pool(name="work", bufs=4))
-        psum = ctx.enter_context(tc.psum_pool(name="psum", bufs=2))
+        psum = ctx.enter_context(tc.psum_pool(name="psum", bufs=1))
         ctx.enter_context(tc.manual_schedule())
 
-        x_groups = [(0, 1), (1, 2), (2, 4), (4, 8)]
-        rnd_groups = [(0, 1), (1, 2), (2, 4)]
-        x_sb = [keep.tile([P, n1 - n0, D], BF16, name="x_sb%d" % n0) for n0, n1 in x_groups]
-        rnd_sb = [keep.tile([P, t1 - t0, S], BF16, name="rnd_sb%d" % t0) for t0, t1 in rnd_groups]
-        w_sb = keep.tile([P, S], U32, name="w_sb", align_bytes=64)
-        wv_sb = keep.tile([P, D], U32, name="wv_sb", align_bytes=64)
-        ws_sb = keep.tile([P, S], U8, name="ws_sb", align_bytes=64)
-        wvs_sb = keep.tile([P, D], U8, name="wvs_sb", align_bytes=64)
+        def mx_tile(name, cols, dtype):
+            tl = keep.tile([P, cols], dtype, name=name, align_bytes=MX_ALIGN)
+            return tl
+
+        x_sb = [keep.tile([P, n1 - n0, D], BF16, name="x_sb%d" % n0) for n0, n1 in X_LOADS]
+        rnd_sb = [keep.tile([P, t1 - t0, S], BF16, name="rnd_sb%d" % t0) for t0, t1 in RND_LOADS]
+        w_sb, ws_sb = mx_tile("w_sb", S, U32), mx_tile("ws_sb", S, U8)
+        wv_sb, wvs_sb = mx_tile("wv_sb", D, U32), mx_tile("wvs_sb", D, U8)
+        xq = [mx_tile("xq%d" % b, S, U32) for b in range(B)]
+        xs = [mx_tile("xs%d" % b, S, U8) for b in range(B)]
+        vq = [mx_tile("vq%d" % b, D, U32) for b in range(B)]
+        vs = [mx_tile("vs%d" % b, D, U8) for b in range(B)]
+        pq, ps = mx_tile("pq", N_TILES * P, U32), mx_tile("ps", N_TILES * P, U8)
+        oq = [mx_tile("oq%d" % b, S, U32) for b in range(B)]
+        os_ = mx_tile("os_", B * S, U8)
+        vn = [keep.tile([P, PACK, D], BF16, name="vn%d" % b, align_bytes=MX_ALIGN) for b in range(B)]
+        og = [keep.tile([P, S, PACK], BF16, name="og%d" % b, align_bytes=MX_ALIGN) for b in range(B)]
         rm = keep.tile([P, TILES, S], F32, name="rm")
+        lg = keep.tile([P, N_TILES, S], F32, name="lg")
+        nmax = keep.tile([P, N_TILES], F32, name="nmax")
+        tot = keep.tile([P, N_TILES], F32, name="tot")
+        rinv = keep.tile([P, N_TILES], F32, name="rinv")
         mix_bf = keep.tile([P, 2], BF16, name="mix_bf")
         u_bf = keep.tile([P, TILES], BF16, name="u_bf")
         u_f = keep.tile([P, TILES], F32, name="u_f")
         c_row = keep.tile([P, S], BF16, name="c_row")
         ones = keep.tile([P, P], BF16, name="ones")
         ident = keep.tile([P, P], F32, name="ident")
-        c_ps = psum.tile([P, S], F32, name="c_ps", bufs=1)
+        c_ps = psum.tile([P, S], F32, name="c_ps")
 
-        xq = [keep.tile([P, S], U32, name="xq%d" % b, align_bytes=64) for b in range(B)]
-        xs = [keep.tile([P, S], U8, name="xs%d" % b, align_bytes=64) for b in range(B)]
-        vn = [keep.tile([P, PACK, D], BF16, name="vn%d" % b, align_bytes=64) for b in range(B)]
-        vq = [keep.tile([P, D], U32, name="vq%d" % b, align_bytes=64) for b in range(B)]
-        vs = [keep.tile([P, D], U8, name="vs%d" % b, align_bytes=64) for b in range(B)]
-        og = [keep.tile([P, S, PACK], BF16, name="og%d" % b, align_bytes=64) for b in range(B)]
-        oq = [keep.tile([P, S], U32, name="oq%d" % b, align_bytes=64) for b in range(B)]
-        os_ = keep.tile([P, B * S], U8, name="os_", align_bytes=64)
-        pq = keep.tile([P, N_TILES * P], U32, name="pq", align_bytes=64)
-        pqs = keep.tile([P, N_TILES * P], U8, name="pqs", align_bytes=64)
-        lg = keep.tile([P, N_TILES, S], F32, name="lg")
-        nmax = keep.tile([P, N_TILES], F32, name="nmax")
-        tot = keep.tile([P, N_TILES], F32, name="tot")
-        rinv = keep.tile([P, N_TILES], F32, name="rinv")
+        held = {}
 
-        state = {}
+        def bank():
+            acc = psum.tile([P, D], F32, name="acc", bufs=ROTATING_BANKS)
+            return acc
 
-        def spread_c():
-            nc.tensor.matmul(
-                c_ps[:], lhsT=ones[:], rhs=c_row[:],
-                start=True, stop=True,
+        def stage(name):
+            tl = keep.tile([P, D * PACK], BF16, name=name, align_bytes=MX_ALIGN)
+            return tl
+
+        def cols(n, cnt=1):
+            return slice(P * n, P * (n + cnt))
+
+        def tile_of(loads, tiles, n):
+            return [tl[:, n - n0, :] for (n0, n1), tl in zip(loads, tiles) if n0 <= n < n1][0]
+
+        def mx_matmul(out, lq, ls, rq, rs):
+            nc.tensor.matmul_mx(
+                out=out, lhsT=lq.bitcast(X4), lhsT_scale=ls, rhs=rq.bitcast(X4), rhs_scale=rs, start=True, stop=True
             )
 
-        def stage(user):
-            tl = keep.tile([P, D, PACK], BF16, name="stage_%s" % "_".join(map(str, SHARES.get(user, user))), align_bytes=64)
-            return tl
+        def quantise(words, scales, src):
+            nc.vector.quantize_mx(out=words.bitcast(X4), scales=scales, in_=src)
+
+        def turn(dst, src):
+            words = src.bitcast(F32)
+            for h in range(PAIR):
+                nc.tensor.transpose(dst[:, h, :], words[:, h : PAIR * P : PAIR], ident[:])
+
+        def turned(acc):
+            return acc[:].rearrange("p (i h n) -> p i h n", i=PAIR, h=PAIR)
 
         def load_rows(dst, rows, t0, t1):
             nc.sync.dma_start(out=dst[:], in_=rows.rearrange("(p t) f -> p t f", t=TILES)[:, t0:t1, :])
 
         def load_x(g):
-            n0, n1 = x_groups[g]
-            b = n0 // TILES
-            load_rows(x_sb[g], x[b], n0 - TILES * b, n1 - TILES * b)
+            b, t0 = divmod(X_LOADS[g][0], TILES)
+            load_rows(x_sb[g], x[b], t0, X_LOADS[g][1] - TILES * b)
 
         def load_rnd(g):
-            load_rows(rnd_sb[g], rnd, *rnd_groups[g])
-
-        def load_scales(dst, src):
-            for q in range(4):
-                nc.sync.dma_start(
-                    out=dst[32 * q : 32 * q + 4, :].bitcast(I32),
-                    in_=src[0, 4 * q : 4 * q + 4, :].bitcast(I32),
-                )
+            load_rows(rnd_sb[g], rnd, *RND_LOADS[g])
 
         def load_words(dst, src):
-            nc.sync.dma_start(
-                out=dst[:].bitcast(I32), in_=src[0].rearrange("p n t -> p (n t)").bitcast(I32)
-            )
+            nc.sync.dma_start(out=dst[:].bitcast(I32), in_=src[0].rearrange("p n t -> p (n t)").bitcast(I32))
 
-        def in_group(groups, tiles, n):
-            for (n0, n1), tl in zip(groups, tiles):
-                if n0 <= n < n1:
-                    return tl[:, n - n0, :]
-
-        def rnd_mix(t, eng):
-            src = in_group(rnd_groups, rnd_sb, t)
-            if eng == "v":
-                nc.vector.tensor_scalar(
-                    out=rm[:, t, :], in0=src, scalar1=mix_bf[:, 1:2], scalar2=None, op0=ALU.mult
-                )
-            else:
-                nc.gpsimd.tensor_scalar(
-                    out=rm[:, t, :], in0=src, scalar1=mix_bf[:, 1:2], scalar2=0.0, op0=ALU.mult, op1=ALU.add
+        def load_scales(dst, src):
+            for q in range(P // QUADRANT):
+                nc.sync.dma_start(
+                    out=dst[QUADRANT * q : QUADRANT * q + SCALE_ROWS, :].bitcast(I32),
+                    in_=src[0, SCALE_ROWS * q : SCALE_ROWS * (q + 1), :].bitcast(I32),
                 )
 
         def x_turn(n, cnt):
-            xt = acc_bank()[:].rearrange("p (i h n) -> p i h n", i=2, h=2)
+            held["xt", n] = turned(bank())
             for i in range(cnt):
-                words = in_group(x_groups, x_sb, n + i).bitcast(F32)
-                for h in range(2):
-                    nc.tensor.transpose(xt[:, i, h, :], words[:, h : 2 * P : 2], ident[:])
-            state["xt", n] = xt
+                turn(held["xt", n][:, i], tile_of(X_LOADS, x_sb, n + i))
 
-        def x_evac(n, cnt, eng="s"):
-            xg = stage(("x", n))[:, 0 : 2 * P].rearrange("p (i n) j -> p i n j", i=2)
-            copier(eng)(
-                out=xg[:, 0:cnt].rearrange("p i n j -> p (i n j)").bitcast(F32).rearrange("p (i n h) -> p i n h", h=2, i=cnt),
-                in_=state["xt", n][:, 0:cnt].rearrange("p i h n -> p i n h"),
+        def x_copy(n, cnt):
+            held["xg", n] = stage("stage_x%d" % n)[:, 0 : cnt * P * PACK]
+            nc.scalar.copy(
+                out=held["xg", n].bitcast(F32).rearrange("p (i n h) -> p i n h", i=cnt, h=PAIR),
+                in_=held["xt", n][:, 0:cnt].rearrange("p i h n -> p i n h"),
             )
-            state["xg", n] = xg
 
         def x_quant(n, cnt):
             b, t = divmod(n, TILES)
-            cols = slice(P * t, P * (t + cnt))
-            nc.vector.quantize_mx(
-                out=xq[b][:, cols].bitcast(X4), scales=xs[b][:, cols],
-                in_=state["xg", n][:, 0:cnt].rearrange("p i n j -> p (i n j)"),
+            quantise(xq[b][:, cols(t, cnt)], xs[b][:, cols(t, cnt)], held["xg", n])
+
+        def rnd_mix_vector(t):
+            nc.vector.tensor_scalar(
+                out=rm[:, t, :], in0=tile_of(RND_LOADS, rnd_sb, t), scalar1=mix_bf[:, 1:2], scalar2=None, op0=ALU.mult
+            )
+
+        def rnd_mix_gpsimd(t):
+            nc.gpsimd.tensor_scalar(
+                out=rm[:, t, :], in0=tile_of(RND_LOADS, rnd_sb, t), scalar1=mix_bf[:, 1:2], scalar2=0.0,
+                op0=ALU.mult, op1=ALU.add,
             )
 
         def syn(n):
             b, t = divmod(n, TILES)
-            cols = slice(P * t, P * (t + 1))
-            ps = acc_bank()
-            nc.tensor.matmul_mx(
-                out=ps[:], lhsT=xq[b][:, cols].bitcast(X4), lhsT_scale=xs[b][:, cols],
-                rhs=w_sb[:].bitcast(X4), rhs_scale=ws_sb[:], start=True, stop=True,
-            )
-            state["syn", n] = ps
+            held["syn", n] = bank()
+            mx_matmul(held["syn", n][:], xq[b][:, cols(t)], xs[b][:, cols(t)], w_sb[:], ws_sb[:])
 
         def logit(n):
             nc.vector.scalar_tensor_tensor(
-                out=lg[:, n, :], in0=state["syn", n][:], scalar=mix_bf[:, 0:1], in1=rm[:, n % TILES, :],
+                out=lg[:, n, :], in0=held["syn", n][:], scalar=mix_bf[:, 0:1], in1=rm[:, n % TILES, :],
                 op0=ALU.mult, op1=ALU.add,
             )
 
-        def row_max(n, cnt):
-            nc.vector.tensor_reduce(
-                out=nmax[:, n : n + cnt], in_=lg[:, n : n + cnt, :], axis=AXIS.X, op=ALU.max, negate=True
-            )
+        def row_max(n):
+            nc.vector.tensor_reduce(out=nmax[:, n : n + 1], in_=lg[:, n, :], axis=AXIS.X, op=ALU.max, negate=True)
 
         def expo(n):
             e = work.tile([P, S], F32, name="e")
             nc.scalar.activation(
-                out=e[:], in_=lg[:, n, :],
-                func=ACT.Exp, bias=nmax[:, n : n + 1], scale=1.0, accum_out=tot[:, n : n + 1],
+                out=e[:], in_=lg[:, n, :], func=ACT.Exp, bias=nmax[:, n : n + 1], scale=1.0,
+                accum_out=tot[:, n : n + 1],
             )
-            state["e", n] = e
+            held["e", n] = e
 
-        def recip(n, cnt):
-            nc.vector.reciprocal(rinv[:, n : n + cnt], tot[:, n : n + cnt])
+        def recip(a):
+            nc.vector.reciprocal(rinv[:, a : a + PAIR], tot[:, a : a + PAIR])
 
-        def pc(n):
-            pcs = work.tile([P, S], BF16, name="pcs", align_bytes=64)
+        def scale_and_turn(n):
+            pc = work.tile([P, S], BF16, name="pc", align_bytes=MX_ALIGN)
             nc.vector.scalar_tensor_tensor(
-                out=pcs[:], in0=state["e", n][:], scalar=rinv[:, n : n + 1], in1=c_ps[:],
-                op0=ALU.mult, op1=ALU.mult,
+                out=pc[:], in0=held["e", n][:], scalar=rinv[:, n : n + 1], in1=c_ps[:], op0=ALU.mult, op1=ALU.mult
             )
-            state["pcs", n] = pcs
+            if n % PAIR == 0:
+                held["pt", n] = turned(bank())
+            turn(held["pt", n - n % PAIR][:, n % PAIR], pc[:])
 
-        def p_turn(n, i=0):
-            if i == 0:
-                state["pt", n] = acc_bank()[:].rearrange("p (i h n) -> p i h n", i=2, h=2)
-            words = state["pcs", n][:].bitcast(F32)
-            for h in range(2):
-                nc.tensor.transpose(state["pt", n - i][:, i, h, :], words[:, h : 2 * P : 2], ident[:])
-
-        def p_evac(n, cnt):
-            pg = stage(("p", n))[:, 0 : cnt * P].rearrange("p n j -> p (n j)")
+        def p_copy(a):
+            held["pg", a] = stage("stage_p%d" % a)[:, 0 : PAIR * P * PACK]
             nc.scalar.copy(
-                out=pg.bitcast(F32).rearrange("p (n i h) -> p n i h", h=2, i=cnt),
-                in_=state["pt", n][:, 0:cnt].rearrange("p i h n -> p n i h"),
-            )
-            state["pg", n] = pg
-            for i in range(cnt):
-                state["rows", n + i] = (slice(P // cnt * i, P // cnt * (i + 1)), slice(n % TILES, n % TILES + cnt))
-
-        def p_quant(n, cnt):
-            cols = slice(P * n, P * (n + cnt))
-            nc.vector.quantize_mx(
-                out=pq[:, cols].bitcast(X4), scales=pqs[:, cols],
-                in_=state["pg", n],
+                out=held["pg", a].bitcast(F32).rearrange("p (n i h) -> p n i h", i=PAIR, h=PAIR),
+                in_=held["pt", a].rearrange("p i h n -> p n i h"),
             )
 
-        def acc_bank():
-            acc = psum.tile([P, D], F32, name="acc", bufs=7)
-            return acc
-
-        def warm_up(cnt):
-            junk = acc_bank()
-            for i in range(cnt):
-                nc.tensor.matmul(junk[:], lhsT=c_row[:, 0:P], rhs=c_row[:], start=True, stop=True)
+        def p_quant(a):
+            quantise(pq[:, cols(a, PAIR)], ps[:, cols(a, PAIR)], held["pg", a])
 
         def v_mm(n):
             b, t = divmod(n, TILES)
-            cols = slice(P * t, P * (t + 1))
-            ps = acc_bank()
-            nc.tensor.matmul_mx(
-                out=ps[:], lhsT=xq[b][:, cols].bitcast(X4), lhsT_scale=xs[b][:, cols],
-                rhs=wv_sb[:].bitcast(X4), rhs_scale=wvs_sb[:], start=True, stop=True,
-            )
-            state["vps", n] = ps
+            held["v", n] = bank()
+            mx_matmul(held["v", n][:], xq[b][:, cols(t)], xs[b][:, cols(t)], wv_sb[:], wvs_sb[:])
 
         def v_gain(n):
             b, t = divmod(n, TILES)
             nc.scalar.activation(
-                out=vn[b][:, t, :].rearrange("p (d m) -> p d m", d=PACK),
-                in_=state["vps", n][:].rearrange("p (m d) -> p d m", d=PACK),
+                out=vn[b][:, t, :].rearrange("p (j m) -> p j m", j=PACK),
+                in_=held["v", n][:].rearrange("p (m j) -> p j m", j=PACK),
                 func=ACT.Copy, scale=u_f[:, t : t + 1],
             )
 
-        def v_pack(b):
-            vg = stage(("v", b))
+        def v_pack(b, after):
+            held["vg", b] = stage(after)[:]
             nc.gpsimd.tensor_scalar(
-                out=vg[:], in0=vn[b][:].rearrange("p t c -> p c t"),
+                out=held["vg", b].rearrange("p (c t) -> p c t", t=PACK), in0=vn[b][:].rearrange("p t c -> p c t"),
                 scalar1=1.0, scalar2=0.0, op0=ALU.mult, op1=ALU.add,
             )
-            state["vg", b] = vg
 
         def v_quant(b):
-            nc.vector.quantize_mx(
-                out=vq[b][:].bitcast(X4), scales=vs[b][:], in_=state["vg", b][:].rearrange("p n j -> p (n j)")
-            )
+            quantise(vq[b][:], vs[b][:], held["vg", b])
 
-        def nat_mm(n):
+        def unit_tokens(n):
+            half, t0 = n % PAIR, n % TILES - n % PAIR
+            return slice(P // PAIR * half, P // PAIR * (half + 1)), slice(t0, t0 + PAIR)
+
+        def rows_mm(n):
             b = n // TILES
-            nat = acc_bank()
-            nc.tensor.matmul_mx(
-                out=nat[:], lhsT=pq[:, P * n : P * (n + 1)].bitcast(X4), lhsT_scale=pqs[:, P * n : P * (n + 1)],
-                rhs=vq[b][:].bitcast(X4), rhs_scale=vs[b][:], start=True, stop=True,
-            )
-            state["nat", n] = nat
+            held["rows", n] = bank()
+            mx_matmul(held["rows", n][:], pq[:, cols(n)], ps[:, cols(n)], vq[b][:], vs[b][:])
 
-        def quad_mm(n, p0, p1):
+        def planes_mm(n):
             b = n // TILES
-            qd = acc_bank()
-            w = p1 - p0
-            for d in range(PACK):
-                cols = slice(P * d, P * (d + 1))
-                nc.tensor.matmul_mx(
-                    out=qd[:, w * d : w * (d + 1)], lhsT=vq[b][:, cols].bitcast(X4), lhsT_scale=vs[b][:, cols],
-                    rhs=pq[:, P * n + p0 : P * n + p1].bitcast(X4), rhs_scale=pqs[:, P * n + p0 : P * n + p1], start=True, stop=True,
-                )
-            state["qd", n, p0] = qd
+            held["planes", n] = bank()
+            for j in range(PACK):
+                mx_matmul(held["planes", n][:, cols(j)], vq[b][:, cols(j)], vs[b][:, cols(j)], pq[:, cols(n)], ps[:, cols(n)])
 
-        def quad_mm_last(i, half):
-            if i == 0:
-                state["qd", 6 + half, 0] = acc_bank()
-            qd = state["qd", 6 + half, 0][:].rearrange("m (d i p) -> m d i p", d=PACK, i=PAIR)
-            w = P // PAIR
-            cols = slice(P * (6 + i) + w * half, P * (6 + i) + w * (half + 1))
-            for d in range(PACK):
-                fcols = slice(P * d, P * (d + 1))
-                nc.tensor.matmul_mx(
-                    out=qd[:, d, i, :], lhsT=vq[1][:, fcols].bitcast(X4), lhsT_scale=vs[1][:, fcols],
-                    rhs=pq[:, cols].bitcast(X4), rhs_scale=pqs[:, cols], start=True, stop=True,
-                )
-
-        def quad_evac_last(half, eng):
-            w = P // PAIR
-            copier(eng)(
-                out=og[1][:].rearrange("m (p t) d -> m p t d", t=TILES)[:, w * half : w * (half + 1), 2:4, :],
-                in_=state["qd", 6 + half, 0][:].rearrange("m (d i p) -> m p i d", d=PACK, i=PAIR),
-            )
-
-        def copier(eng):
-            return nc.scalar.copy if eng == "s" else nc.vector.tensor_copy
-
-        def nat_evac(n, eng):
-            b, t = divmod(n, TILES)
+        def rows_out(n, queue):
             ob = work.tile([P, D], F32, name="ob")
-            copier(eng)(
-                out=ob[:].rearrange("p (m d) -> p m d", d=PACK),
-                in_=state["nat", n][:].rearrange("p (d m) -> p m d", d=PACK),
+            nc.scalar.copy(
+                out=ob[:].rearrange("p (m j) -> p m j", j=PACK),
+                in_=held["rows", n][:].rearrange("p (j m) -> p m j", j=PACK),
             )
-            ps, ts = state["rows", n]
-            nc.sync.dma_start(out=out_0[b].rearrange("(p t) d -> p t d", t=TILES)[ps, ts, :], in_=ob[:])
+            parts, tiles = unit_tokens(n)
+            queue.dma_start(out=out_0[n // TILES].rearrange("(p t) d -> p t d", t=TILES)[parts, tiles, :], in_=ob[:])
 
-        def quad_evac(n, p0, p1, eng):
-            ps, ts = state["rows", n]
-            copier(eng)(
-                out=og[n // TILES][:].rearrange("m (p t) d -> m p t d", t=TILES)[:, ps, ts, :],
-                in_=state["qd", n, p0][:].rearrange("m (d p i) -> m p i d", d=PACK, i=ts.stop - ts.start),
+        def planes_copy(n, copy):
+            parts, tiles = unit_tokens(n)
+            copy(
+                out=og[n // TILES][:].rearrange("m (p t) j -> m p t j", t=TILES)[:, parts, tiles, :],
+                in_=held["planes", n][:].rearrange("m (j p i) -> m p i j", j=PACK, i=PAIR),
             )
 
-        def o_quant(b, i0, i1):
-            nc.vector.quantize_mx(
-                out=oq[b][:, i0:i1].bitcast(X4), scales=os_[:, S * b + i0 : S * b + i1],
-                in_=og[b][:, i0:i1, :].rearrange("m i d -> m (i d)"),
-            )
+        def planes_out(b, half):
+            here = slice(HALF * half, HALF * (half + 1))
+            there = slice(S * b + here.start, S * b + here.stop)
+            quantise(oq[b][:, here], os_[:, there], og[b][:, here, :].rearrange("m s j -> m (s j)"))
             nc.sync.dma_start(
-                out=out_1[0][:, S * b + i0 : S * b + i1, :].rearrange("m i d -> m (i d)").bitcast(I32),
-                in_=oq[b][:, i0:i1].bitcast(I32),
+                out=out_1[0][:, there, :].rearrange("m s j -> m (s j)").bitcast(I32), in_=oq[b][:, here].bitcast(I32)
             )
 
-        def o_scales():
-            for q in range(4):
-                nc.sync.dma_start(
-                    out=out_2[0, 4 * q : 4 * q + 4, :].bitcast(I32), in_=os_[32 * q : 32 * q + 4, :].bitcast(I32)
-                )
+        def warm_up():
+            unread = bank()
+            for _ in range(WARM_UPS):
+                nc.tensor.matmul(unread[:], lhsT=c_row[:, 0:P], rhs=c_row[:], start=True, stop=True)
+
+        def softmax_front(a):
+            logit(a)
+            logit(a + 1)
+            row_max(a)
+            recip(a - PAIR)
+            row_max(a + 1)
+
+        on_scalar, on_vector = nc.scalar.copy, nc.vector.tensor_copy
 
         nc.vector.memset(ws_sb[:].bitcast(I32), 0)
         nc.vector.memset(c_row[:], 0.0)
@@ -328,9 +275,8 @@ def tile_mixturedenserandomsynthesizer_x2_kernel(
         nc.gpsimd.dma_start(out=mix_bf[:], in_=mix.partition_broadcast(P))
         make_identity(nc, ident[:])
         nc.scalar.activation(out=ones[:], in_=c_row[:, 0:P], func=ACT.Copy, bias=1.0)
-        load_x(0)
-        load_x(1)
-        load_x(2)
+        for g in range(3):
+            load_x(g)
         load_scales(ws_sb, w_scales)
         load_words(w_sb, w_words)
         nc.gpsimd.dma_start(out=u_bf[:], in_=u.rearrange("(p t) -> p t", t=TILES))
@@ -342,144 +288,123 @@ def tile_mixturedenserandomsynthesizer_x2_kernel(
         nc.sync.dma_start(out=c_row[0:1, :], in_=c.rearrange("(o k) -> o k", o=1))
         load_x(3)
 
-        x_turn(0, 1)
-        x_turn(1, 1)
-        x_turn(2, 2)
-        x_evac(0, 1)
-        x_evac(1, 1)
-        x_evac(2, 2)
-        x_quant(0, 1)
-        syn(0)
-        x_quant(1, 1)
-        rnd_mix(0, "v")
-        syn(1)
-        rnd_mix(1, "v")
+        for n0, n1 in X_LOADS[:3]:
+            x_turn(n0, n1 - n0)
+        for n0, n1 in X_LOADS[:3]:
+            x_copy(n0, n1 - n0)
         nc.scalar.copy(out=u_f[:], in_=u_bf[:])
-        rnd_mix(2, "g")
-        rnd_mix(3, "g")
-        v_mm(0)
-        v_mm(1)
+        for n in range(PAIR):
+            x_quant(n, 1)
+            syn(n)
+        for n in range(PAIR):
+            rnd_mix_vector(n)
+            rnd_mix_gpsimd(PAIR + n)
+            v_mm(n)
         logit(0)
-        x_quant(2, 2)
+        x_quant(2, PAIR)
         syn(2)
         v_mm(2)
         logit(1)
         v_gain(0)
         v_mm(3)
         syn(3)
-        spread_c()
-        row_max(0, 1)
-        v_gain(1)
-        expo(0)
-        x_turn(4, 2)
-        row_max(1, 1)
-        v_gain(2)
-        x_turn(6, 2)
-        expo(1)
-        logit(2)
-        logit(3)
-        row_max(2, 1)
-        recip(0, 2)
-        row_max(3, 1)
-        x_evac(4, 2)
-        x_evac(6, 2)
+        nc.tensor.matmul(c_ps[:], lhsT=ones[:], rhs=c_row[:], start=True, stop=True)
+        for n in range(PAIR):
+            row_max(n)
+            v_gain(n + 1)
+            expo(n)
+            x_turn(TILES + PAIR * n, PAIR)
+
+        softmax_front(2)
+        x_copy(4, PAIR)
+        x_copy(6, PAIR)
         v_gain(3)
-        x_quant(4, 2)
-        warm_up(2)
+        x_quant(4, PAIR)
+        warm_up()
         syn(4)
         v_mm(4)
         syn(5)
-        x_quant(6, 2)
-        v_pack(0)
-        pc(0)
+        x_quant(6, PAIR)
+        v_pack(0, "stage_x6")
         v_mm(5)
-        p_turn(0)
-        pc(1)
-        p_turn(1, 1)
+        scale_and_turn(0)
+        scale_and_turn(1)
         v_mm(6)
         v_mm(7)
         expo(2)
         expo(3)
         v_gain(4)
         v_gain(5)
-        p_evac(0, 2)
-        logit(4)
+        p_copy(0)
+
+        softmax_front(4)
         syn(6)
-        logit(5)
         syn(7)
-        row_max(4, 1)
-        recip(2, 2)
-        row_max(5, 1)
         v_quant(0)
-        p_quant(0, 2)
+        p_quant(0)
         v_gain(6)
         v_gain(7)
-        v_pack(1)
-        warm_up(2)
-        nat_mm(0)
-        quad_mm(0, 0, P)
-        pc(2)
-        p_turn(2)
-        pc(3)
-        p_turn(3, 1)
-        nat_mm(1)
-        quad_mm(1, 0, P)
+        v_pack(1, "stage_p0")
+        warm_up()
+        rows_mm(0)
+        rows_mm(1)
+        scale_and_turn(2)
+        scale_and_turn(3)
+        planes_mm(0)
+        planes_mm(1)
         expo(4)
         expo(5)
-        nat_evac(0, "s")
-        quad_evac(0, 0, P, "s")
-        p_evac(2, 2)
-        logit(6)
-        recip(4, 2)
-        logit(7)
-        pc(4)
-        p_turn(4)
-        row_max(6, 1)
-        p_quant(2, 2)
-        warm_up(1)
-        nat_mm(2)
-        quad_mm(2, 0, P)
-        row_max(7, 1)
-        pc(5)
-        p_turn(5, 1)
-        nat_mm(3)
-        quad_mm(3, 0, P)
-        nat_evac(1, "s")
+        rows_out(0, nc.sync)
+        rows_out(1, nc.sync)
+        p_copy(2)
+
+        softmax_front(6)
+        p_quant(2)
+        warm_up()
+        rows_mm(2)
+        rows_mm(3)
+        scale_and_turn(4)
+        scale_and_turn(5)
+        planes_copy(0, on_scalar)
         expo(6)
-        quad_evac(1, 0, P, "s")
         expo(7)
+        planes_copy(1, on_scalar)
+        planes_mm(2)
+        planes_mm(3)
+        recip(6)
         v_quant(1)
-        nat_evac(2, "s")
-        p_evac(4, 2)
-        recip(6, 2)
-        pc(6)
-        warm_up(1)
-        p_turn(6)
-        pc(7)
-        p_turn(7, 1)
-        p_quant(4, 2)
-        nat_mm(4)
-        quad_evac(2, 0, P, "s")
-        nat_mm(5)
-        quad_evac(3, 0, P, "s")
-        quad_mm(4, 0, P)
-        quad_mm(5, 0, P)
-        p_evac(6, 2)
-        nat_evac(3, "v")
-        o_quant(0, 0, S)
-        p_quant(6, 2)
-        nat_evac(4, "s")
-        nat_mm(6)
-        quad_mm(6, 0, P)
-        nat_evac(5, "s")
-        nat_mm(7)
-        quad_evac(4, 0, P, "v")
-        quad_mm(7, 0, P)
-        quad_evac(5, 0, P, "v")
-        nat_evac(6, "s")
-        nat_evac(7, "s")
-        quad_evac(6, 0, P, "v")
-        quad_evac(7, 0, P, "v")
-        o_quant(1, 0, S // 2)
-        o_quant(1, S // 2, S)
-        o_scales()
+        rows_out(2, nc.sync)
+        p_copy(4)
+        rows_out(3, nc.sync)
+
+        scale_and_turn(6)
+        scale_and_turn(7)
+        p_quant(4)
+        rows_mm(4)
+        rows_mm(5)
+        planes_copy(2, on_scalar)
+        planes_copy(3, on_vector)
+        planes_mm(4)
+        planes_mm(5)
+        p_copy(6)
+        for half in range(PAIR):
+            planes_out(0, half)
+        p_quant(6)
+        rows_out(4, nc.sync)
+        rows_mm(6)
+        rows_out(5, nc.sync)
+        for n in (4, 5):
+            planes_mm(n + PAIR)
+            planes_copy(n, on_vector)
+        rows_mm(7)
+        rows_out(6, nc.sync)
+        planes_copy(6, on_vector)
+        planes_copy(7, on_scalar)
+        for half in range(PAIR):
+            planes_out(1, half)
+        for q in range(P // QUADRANT):
+            nc.sync.dma_start(
+                out=out_2[0, SCALE_ROWS * q : SCALE_ROWS * (q + 1), :].bitcast(I32),
+                in_=os_[QUADRANT * q : QUADRANT * q + SCALE_ROWS, :].bitcast(I32),
+            )
+        rows_out(7, nc.scalar)

@@ -340,8 +340,8 @@ def tile_mixturedenserandomsynthesizer_x2_kernel(
         softmax_front(4)
         syn(6)
         syn(7)
-        v_quant(0)
         p_quant(0)
+        v_quant(0)
         v_gain(6)
         v_gain(7)
         v_pack(1, "stage_p0")

@@ -25,7 +25,7 @@ HALF = S // 2
 QUADRANT, SCALE_ROWS = 32, 4
 MX_ALIGN = 64
 ROTATING_BANKS = 7
-WARM_UPS = 2
+WARM_WIDTH = 256
 X_LOADS = ((0, 1), (1, 2), (2, 4), (4, 8))
 RND_LOADS = ((0, 1), (1, 2), (2, 4))
 
@@ -63,9 +63,11 @@ def tile_mixturedenserandomsynthesizer_x2_kernel(
         tot = keep.tile([P, N_TILES], F32, name="tot")
         rinv = keep.tile([P, N_TILES], F32, name="rinv")
         mix_bf = keep.tile([P, 2], BF16, name="mix_bf")
+        mix_f = keep.tile([P, 2], F32, name="mix_f")
         u_bf = keep.tile([P, TILES], BF16, name="u_bf")
         u_f = keep.tile([P, TILES], F32, name="u_f")
         c_row = keep.tile([P, S], BF16, name="c_row")
+        zeros = keep.tile([P, S], BF16, name="zeros")
         ones = keep.tile([P, P], BF16, name="ones")
         ident = keep.tile([P, P], F32, name="ident")
         c_ps = psum.tile([P, S], F32, name="c_ps")
@@ -116,11 +118,8 @@ def tile_mixturedenserandomsynthesizer_x2_kernel(
             nc.sync.dma_start(out=dst[:].bitcast(I32), in_=src[0].rearrange("p n t -> p (n t)").bitcast(I32))
 
         def load_scales(dst, src):
-            for q in range(P // QUADRANT):
-                nc.sync.dma_start(
-                    out=dst[QUADRANT * q : QUADRANT * q + SCALE_ROWS, :].bitcast(I32),
-                    in_=src[0, SCALE_ROWS * q : SCALE_ROWS * (q + 1), :].bitcast(I32),
-                )
+            for r in range(SCALE_ROWS):
+                nc.sync.dma_start(out=dst[r:P:QUADRANT, :].bitcast(I32), in_=src[0, r::SCALE_ROWS, :].bitcast(I32))
 
         def x_turn(n, cnt):
             held["xt", n] = turned(bank())
@@ -142,6 +141,9 @@ def tile_mixturedenserandomsynthesizer_x2_kernel(
             nc.vector.tensor_scalar(
                 out=rm[:, t, :], in0=tile_of(RND_LOADS, rnd_sb, t), scalar1=mix_bf[:, 1:2], scalar2=None, op0=ALU.mult
             )
+
+        def rnd_mix_scalar(t):
+            nc.scalar.activation(out=rm[:, t, :], in_=tile_of(RND_LOADS, rnd_sb, t), func=ACT.Copy, scale=mix_f[:, 1:2])
 
         def rnd_mix_gpsimd(t):
             nc.gpsimd.tensor_scalar(
@@ -175,13 +177,20 @@ def tile_mixturedenserandomsynthesizer_x2_kernel(
             nc.vector.reciprocal(rinv[:, a : a + PAIR], tot[:, a : a + PAIR])
 
         def scale_and_turn(n):
+            scale(n)
+            p_turn(n)
+
+        def scale(n):
             pc = work.tile([P, S], BF16, name="pc", align_bytes=MX_ALIGN)
             nc.vector.scalar_tensor_tensor(
                 out=pc[:], in0=held["e", n][:], scalar=rinv[:, n : n + 1], in1=c_ps[:], op0=ALU.mult, op1=ALU.mult
             )
+            held["pc", n] = pc
+
+        def p_turn(n):
             if n % PAIR == 0:
                 held["pt", n] = turned(bank())
-            turn(held["pt", n - n % PAIR][:, n % PAIR], pc[:])
+            turn(held["pt", n - n % PAIR][:, n % PAIR], held["pc", n][:])
 
         def p_copy(a):
             held["pg", a] = stage("stage_p%d" % a)[:, 0 : PAIR * P * PACK]
@@ -189,6 +198,17 @@ def tile_mixturedenserandomsynthesizer_x2_kernel(
                 out=held["pg", a].bitcast(F32).rearrange("p (n i h) -> p n i h", i=PAIR, h=PAIR),
                 in_=held["pt", a].rearrange("p i h n -> p n i h"),
             )
+
+        def p_copy_unit(n):
+            a, half = n - n % PAIR, slice(P // PAIR * (n % PAIR), P // PAIR * (n % PAIR + 1))
+            held["pg1", n] = stage("stage_u%d" % n)[:, 0 : P * PACK]
+            nc.scalar.copy(
+                out=held["pg1", n].bitcast(F32).rearrange("p (n i h) -> p n i h", i=PAIR, h=PAIR),
+                in_=held["pt", a].rearrange("p i h n -> p n i h")[:, half],
+            )
+
+        def p_quant_unit(n):
+            quantise(pq[:, cols(n)], ps[:, cols(n)], held["pg1", n])
 
         def p_quant(a):
             quantise(pq[:, cols(a, PAIR)], ps[:, cols(a, PAIR)], held["pg", a])
@@ -231,12 +251,13 @@ def tile_mixturedenserandomsynthesizer_x2_kernel(
             for j in range(PACK):
                 mx_matmul(held["planes", n][:, cols(j)], vq[b][:, cols(j)], vs[b][:, cols(j)], pq[:, cols(n)], ps[:, cols(n)])
 
-        def rows_out(n, queue):
+        def rows_out(n, queue, copy=nc.scalar.copy):
             ob = work.tile([P, D], F32, name="ob")
-            nc.scalar.copy(
+            copy(
                 out=ob[:].rearrange("p (m j) -> p m j", j=PACK),
                 in_=held["rows", n][:].rearrange("p (j m) -> p m j", j=PACK),
             )
+            held["ob", n] = ob
             parts, tiles = unit_tokens(n)
             queue.dma_start(out=out_0[n // TILES].rearrange("(p t) d -> p t d", t=TILES)[parts, tiles, :], in_=ob[:])
 
@@ -247,33 +268,63 @@ def tile_mixturedenserandomsynthesizer_x2_kernel(
                 in_=held["planes", n][:].rearrange("m (j p i) -> m p i j", j=PACK, i=PAIR),
             )
 
-        def planes_out(b, half):
+        def rows_round(n, buffer):
+            held["oc", n] = stage(buffer)[:, 0:D]
+            nc.gpsimd.tensor_scalar(
+                out=held["oc", n], in0=held["ob", n][:], scalar1=1.0, scalar2=0.0, op0=ALU.mult, op1=ALU.add
+            )
+
+        def rows_turn(n):
+            if n % PAIR == 0:
+                held["ot", n] = turned(bank())
+            turn(held["ot", n - n % PAIR][:, n % PAIR], held["oc", n])
+
+        def rows_turned_copy(a, copy):
+            t0 = a % TILES
+            words = og[a // TILES][:].rearrange("m s j -> m (s j)").bitcast(F32)
+            copy(
+                out=words.rearrange("m (g p t h) -> m g p t h", g=PAIR, t=TILES, h=PAIR)[:, :, :, t0 : t0 + PAIR, :],
+                in_=held["ot", a].rearrange("m g h (p i) -> m g p i h", i=PAIR),
+            )
+
+        def planes_quant(b, half):
             here = slice(HALF * half, HALF * (half + 1))
             there = slice(S * b + here.start, S * b + here.stop)
             quantise(oq[b][:, here], os_[:, there], og[b][:, here, :].rearrange("m s j -> m (s j)"))
+
+        def planes_out(b, half):
+            planes_quant(b, half)
+            codes_out(b, slice(HALF * half, HALF * (half + 1)))
+
+        def codes_out(b, here):
+            there = slice(S * b + here.start, S * b + here.stop)
             nc.sync.dma_start(
                 out=out_1[0][:, there, :].rearrange("m s j -> m (s j)").bitcast(I32), in_=oq[b][:, here].bitcast(I32)
             )
 
-        def warm_up():
-            unread = bank()
-            for _ in range(WARM_UPS):
-                nc.tensor.matmul(unread[:], lhsT=c_row[:, 0:P], rhs=c_row[:], start=True, stop=True)
+        def scales_out(there, queue):
+            for r in range(SCALE_ROWS):
+                queue.dma_start(
+                    out=out_2[0, r::SCALE_ROWS, there].bitcast(I32), in_=os_[r:P:QUADRANT, there].bitcast(I32)
+                )
 
-        def softmax_front(a):
-            logit(a)
-            logit(a + 1)
-            row_max(a)
-            recip(a - PAIR)
-            row_max(a + 1)
+        def warm_up(after):
+            unread = bank()
+            nc.tensor.matmul(unread[:, 0:WARM_WIDTH], lhsT=ident[:], rhs=after[:, 0:WARM_WIDTH], start=True, stop=True)
+
+        def head_warm_up(count):
+            unread = bank()
+            for _ in range(count):
+                nc.tensor.matmul(unread[:], lhsT=zeros[:, 0:P], rhs=zeros[:], start=True, stop=True)
 
         on_scalar, on_vector = nc.scalar.copy, nc.vector.tensor_copy
 
+        nc.vector.memset(zeros[:], 0.0)
         nc.vector.memset(ws_sb[:].bitcast(I32), 0)
         nc.vector.memset(c_row[:], 0.0)
         nc.vector.memset(wvs_sb[:].bitcast(I32), 0)
-        nc.gpsimd.dma_start(out=mix_bf[:], in_=mix.partition_broadcast(P))
         make_identity(nc, ident[:])
+        nc.gpsimd.dma_start(out=mix_bf[:], in_=mix.partition_broadcast(P))
         nc.scalar.activation(out=ones[:], in_=c_row[:, 0:P], func=ACT.Copy, bias=1.0)
         for g in range(3):
             load_x(g)
@@ -288,8 +339,10 @@ def tile_mixturedenserandomsynthesizer_x2_kernel(
         nc.sync.dma_start(out=c_row[0:1, :], in_=c.rearrange("(o k) -> o k", o=1))
         load_x(3)
 
-        for n0, n1 in X_LOADS[:3]:
-            x_turn(n0, n1 - n0)
+        head_warm_up(2)
+        x_turn(0, 1)
+        x_turn(1, 1)
+        x_turn(2, PAIR)
         for n0, n1 in X_LOADS[:3]:
             x_copy(n0, n1 - n0)
         nc.scalar.copy(out=u_f[:], in_=u_bf[:])
@@ -315,12 +368,16 @@ def tile_mixturedenserandomsynthesizer_x2_kernel(
             expo(n)
             x_turn(TILES + PAIR * n, PAIR)
 
-        softmax_front(2)
+        logit(2)
+        logit(3)
+        row_max(2)
+        recip(0)
+        row_max(3)
         x_copy(4, PAIR)
         x_copy(6, PAIR)
         v_gain(3)
         x_quant(4, PAIR)
-        warm_up()
+        warm_up(lg[:, 3, :])
         syn(4)
         v_mm(4)
         syn(5)
@@ -337,74 +394,83 @@ def tile_mixturedenserandomsynthesizer_x2_kernel(
         v_gain(5)
         p_copy(0)
 
-        softmax_front(4)
+        logit(4)
+        logit(5)
+        row_max(4)
+        recip(2)
+        row_max(5)
         syn(6)
         syn(7)
+        warm_up(lg[:, 5, :])
         p_quant(0)
         v_quant(0)
         v_gain(6)
         v_gain(7)
         v_pack(1, "stage_p0")
-        warm_up()
         rows_mm(0)
         rows_mm(1)
         scale_and_turn(2)
         scale_and_turn(3)
-        planes_mm(0)
-        planes_mm(1)
         expo(4)
         expo(5)
         rows_out(0, nc.sync)
         rows_out(1, nc.sync)
+        rows_round(0, "stage_o0")
         p_copy(2)
 
-        softmax_front(6)
+        logit(6)
+        warm_up(lg[:, 6, :])
+        logit(7)
+        row_max(6)
+        recip(4)
+        row_max(7)
         p_quant(2)
-        warm_up()
+        rows_round(1, "stage_p2")
+        rows_turn(0)
         rows_mm(2)
+        planes_mm(2)
         rows_mm(3)
         scale_and_turn(4)
         scale_and_turn(5)
-        planes_copy(0, on_scalar)
         expo(6)
         expo(7)
-        planes_copy(1, on_scalar)
-        planes_mm(2)
+        rows_turn(1)
         planes_mm(3)
+        warm_up(lg[:, 7, :])
         recip(6)
         v_quant(1)
         rows_out(2, nc.sync)
+        planes_copy(2, on_scalar)
         p_copy(4)
+        rows_turned_copy(0, on_scalar)
         rows_out(3, nc.sync)
 
         scale_and_turn(6)
         scale_and_turn(7)
         p_quant(4)
         rows_mm(4)
-        rows_mm(5)
-        planes_copy(2, on_scalar)
-        planes_copy(3, on_vector)
         planes_mm(4)
+        rows_mm(5)
+        planes_copy(3, on_vector)
         planes_mm(5)
-        p_copy(6)
-        for half in range(PAIR):
-            planes_out(0, half)
-        p_quant(6)
+        p_copy_unit(6)
+        p_copy_unit(7)
+        planes_out(0, 0)
+        p_quant_unit(6)
+        planes_out(0, 1)
+        p_quant_unit(7)
         rows_out(4, nc.sync)
+        planes_mm(6)
         rows_mm(6)
-        rows_out(5, nc.sync)
-        for n in (4, 5):
-            planes_mm(n + PAIR)
-            planes_copy(n, on_vector)
+        planes_mm(7)
         rows_mm(7)
-        rows_out(6, nc.sync)
+        rows_out(5, nc.sync)
+        planes_copy(4, on_vector)
         planes_copy(6, on_vector)
+        planes_copy(5, on_vector)
+        rows_out(6, nc.sync)
         planes_copy(7, on_scalar)
-        for half in range(PAIR):
-            planes_out(1, half)
-        for q in range(P // QUADRANT):
-            nc.sync.dma_start(
-                out=out_2[0, SCALE_ROWS * q : SCALE_ROWS * (q + 1), :].bitcast(I32),
-                in_=os_[QUADRANT * q : QUADRANT * q + SCALE_ROWS, :].bitcast(I32),
-            )
+        planes_out(1, 0)
+        planes_out(1, 1)
+        scales_out(slice(0, B * S), nc.sync)
         rows_out(7, nc.scalar)

@@ -67,7 +67,6 @@ def tile_mixturedenserandomsynthesizer_x2_kernel(
         u_bf = keep.tile([P, TILES], BF16, name="u_bf")
         u_f = keep.tile([P, TILES], F32, name="u_f")
         c_row = keep.tile([P, S], BF16, name="c_row")
-        zeros = keep.tile([P, S], BF16, name="zeros")
         ones = keep.tile([P, P], BF16, name="ones")
         ident = keep.tile([P, P], F32, name="ident")
         c_ps = psum.tile([P, S], F32, name="c_ps")
@@ -136,11 +135,6 @@ def tile_mixturedenserandomsynthesizer_x2_kernel(
         def x_quant(n, cnt):
             b, t = divmod(n, TILES)
             quantise(xq[b][:, cols(t, cnt)], xs[b][:, cols(t, cnt)], held["xg", n])
-
-        def rnd_mix_vector(t):
-            nc.vector.tensor_scalar(
-                out=rm[:, t, :], in0=tile_of(RND_LOADS, rnd_sb, t), scalar1=mix_bf[:, 1:2], scalar2=None, op0=ALU.mult
-            )
 
         def rnd_mix_scalar(t):
             nc.scalar.activation(out=rm[:, t, :], in_=tile_of(RND_LOADS, rnd_sb, t), func=ACT.Copy, scale=mix_f[:, 1:2])
@@ -274,18 +268,17 @@ def tile_mixturedenserandomsynthesizer_x2_kernel(
                 out=held["oc", n], in0=held["ob", n][:], scalar1=1.0, scalar2=0.0, op0=ALU.mult, op1=ALU.add
             )
 
-        def rows_turn(n):
-            if n % PAIR == 0:
-                held["ot", n] = turned(bank())
-            turn(held["ot", n - n % PAIR][:, n % PAIR], held["oc", n])
-
-        def rows_turned_copy(a, copy):
-            t0 = a % TILES
-            words = og[a // TILES][:].rearrange("m s j -> m (s j)").bitcast(F32)
+        def rows_turned_unit(n, copy):
+            parts, tiles = unit_tokens(n)
+            words = og[n // TILES][:].rearrange("m s j -> m (s j)").bitcast(F32)
             copy(
-                out=words.rearrange("m (g p t h) -> m g p t h", g=PAIR, t=TILES, h=PAIR)[:, :, :, t0 : t0 + PAIR, :],
-                in_=held["ot", a].rearrange("m g h (p i) -> m g p i h", i=PAIR),
+                out=words.rearrange("m (p t h) -> m p t h", t=TILES, h=PAIR)[:, parts, tiles, :],
+                in_=held["ot1", n].rearrange("m h (p i) -> m p i h", i=PAIR),
             )
+
+        def rows_turn_unit(n):
+            held["ot1", n] = turned(bank())[:, 0]
+            turn(held["ot1", n], held["oc", n])
 
         def planes_quant(b, half):
             here = slice(HALF * half, HALF * (half + 1))
@@ -315,16 +308,15 @@ def tile_mixturedenserandomsynthesizer_x2_kernel(
         def head_warm_up(count):
             unread = bank()
             for _ in range(count):
-                nc.tensor.matmul(unread[:], lhsT=zeros[:, 0:P], rhs=zeros[:], start=True, stop=True)
+                nc.tensor.matmul(unread[:], lhsT=c_row[:, 0:P], rhs=c_row[:], start=True, stop=True)
 
         on_scalar, on_vector = nc.scalar.copy, nc.vector.tensor_copy
 
-        nc.vector.memset(zeros[:], 0.0)
-        nc.vector.memset(ws_sb[:].bitcast(I32), 0)
         nc.vector.memset(c_row[:], 0.0)
+        nc.vector.memset(ws_sb[:].bitcast(I32), 0)
         nc.vector.memset(wvs_sb[:].bitcast(I32), 0)
-        make_identity(nc, ident[:])
         nc.gpsimd.dma_start(out=mix_bf[:], in_=mix.partition_broadcast(P))
+        make_identity(nc, ident[:])
         nc.scalar.activation(out=ones[:], in_=c_row[:, 0:P], func=ACT.Copy, bias=1.0)
         for g in range(3):
             load_x(g)
@@ -336,25 +328,28 @@ def tile_mixturedenserandomsynthesizer_x2_kernel(
         load_words(wv_sb, wv_words)
         load_scales(wvs_sb, wv_scales)
         load_rnd(2)
-        nc.sync.dma_start(out=c_row[0:1, :], in_=c.rearrange("(o k) -> o k", o=1))
-        load_x(3)
 
         head_warm_up(2)
+        nc.sync.dma_start(out=c_row[0:1, :], in_=c.rearrange("(o k) -> o k", o=1))
+        load_x(3)
         x_turn(0, 1)
         x_turn(1, 1)
         x_turn(2, PAIR)
-        for n0, n1 in X_LOADS[:3]:
-            x_copy(n0, n1 - n0)
+        x_copy(0, 1)
+        x_copy(1, 1)
+        nc.scalar.copy(out=mix_f[:], in_=mix_bf[:])
+        x_copy(2, PAIR)
+        rnd_mix_scalar(0)
+        rnd_mix_scalar(1)
         nc.scalar.copy(out=u_f[:], in_=u_bf[:])
         for n in range(PAIR):
             x_quant(n, 1)
             syn(n)
         for n in range(PAIR):
-            rnd_mix_vector(n)
             rnd_mix_gpsimd(PAIR + n)
             v_mm(n)
-        logit(0)
         x_quant(2, PAIR)
+        logit(0)
         syn(2)
         v_mm(2)
         logit(1)
@@ -362,12 +357,13 @@ def tile_mixturedenserandomsynthesizer_x2_kernel(
         v_mm(3)
         syn(3)
         nc.tensor.matmul(c_ps[:], lhsT=ones[:], rhs=c_row[:], start=True, stop=True)
-        for n in range(PAIR):
-            row_max(n)
-            v_gain(n + 1)
-            expo(n)
-            x_turn(TILES + PAIR * n, PAIR)
-
+        row_max(0)
+        row_max(1)
+        v_gain(1)
+        expo(0)
+        expo(1)
+        x_turn(4, PAIR)
+        x_turn(6, PAIR)
         logit(2)
         logit(3)
         row_max(2)
@@ -375,6 +371,7 @@ def tile_mixturedenserandomsynthesizer_x2_kernel(
         row_max(3)
         x_copy(4, PAIR)
         x_copy(6, PAIR)
+        v_gain(2)
         v_gain(3)
         x_quant(4, PAIR)
         warm_up(lg[:, 3, :])
@@ -391,8 +388,8 @@ def tile_mixturedenserandomsynthesizer_x2_kernel(
         expo(2)
         expo(3)
         v_gain(4)
-        v_gain(5)
         p_copy(0)
+        v_gain(5)
 
         logit(4)
         logit(5)
@@ -411,11 +408,11 @@ def tile_mixturedenserandomsynthesizer_x2_kernel(
         rows_mm(1)
         scale_and_turn(2)
         scale_and_turn(3)
+        planes_mm(0)
         expo(4)
         expo(5)
         rows_out(0, nc.sync)
         rows_out(1, nc.sync)
-        rows_round(0, "stage_o0")
         p_copy(2)
 
         logit(6)
@@ -426,7 +423,6 @@ def tile_mixturedenserandomsynthesizer_x2_kernel(
         row_max(7)
         p_quant(2)
         rows_round(1, "stage_p2")
-        rows_turn(0)
         rows_mm(2)
         planes_mm(2)
         rows_mm(3)
@@ -434,7 +430,8 @@ def tile_mixturedenserandomsynthesizer_x2_kernel(
         scale_and_turn(5)
         expo(6)
         expo(7)
-        rows_turn(1)
+        planes_copy(0, on_scalar)
+        rows_turn_unit(1)
         planes_mm(3)
         warm_up(lg[:, 7, :])
         recip(6)
@@ -442,7 +439,7 @@ def tile_mixturedenserandomsynthesizer_x2_kernel(
         rows_out(2, nc.sync)
         planes_copy(2, on_scalar)
         p_copy(4)
-        rows_turned_copy(0, on_scalar)
+        rows_turned_unit(1, on_scalar)
         rows_out(3, nc.sync)
 
         scale_and_turn(6)

from contextlib import ExitStack

import concourse.mybir as mybir
from concourse.masks import make_identity

B, S, D = 2, 512, 512
FLOPS = 3 * 2 * B * S * S * D

F32 = mybir.dt.float32
BF16 = mybir.dt.bfloat16
U32 = mybir.dt.uint32
I32 = mybir.dt.int32
U8 = mybir.dt.uint8
X4 = mybir.dt.float8_e4m3fn_x4
ALU = mybir.AluOpType
ACT = mybir.ActivationFunctionType
AXIS = mybir.AxisListType

P = 128
PACK = 4
TILES = S // P
N_TILES = B * TILES
PAIR = 2
HALF = S // 2
QUADRANT, SCALE_ROWS = 32, 4
MX_ALIGN = 64
ROTATING_BANKS = 7
WARM_WIDTH = 256
X_LOADS = ((0, 1), (1, 2), (2, 4), (4, 8))
RND_LOADS = ((0, 1), (1, 2), (2, 4))


def tile_mixturedenserandomsynthesizer_x2_kernel(
    tc, x, w_words, w_scales, rnd, mix, wv_words, wv_scales, c, u, out_0, out_1, out_2
):
    nc = tc.nc
    with ExitStack() as ctx:
        keep = ctx.enter_context(tc.tile_pool(name="keep", bufs=1))
        work = ctx.enter_context(tc.tile_pool(name="work", bufs=4))
        psum = ctx.enter_context(tc.psum_pool(name="psum", bufs=1))
        ctx.enter_context(tc.manual_schedule())

        def mx_tile(name, cols, dtype):
            tl = keep.tile([P, cols], dtype, name=name, align_bytes=MX_ALIGN)
            return tl

        x_sb = [keep.tile([P, n1 - n0, D], BF16, name="x_sb%d" % n0) for n0, n1 in X_LOADS]
        rnd_sb = [keep.tile([P, t1 - t0, S], BF16, name="rnd_sb%d" % t0) for t0, t1 in RND_LOADS]
        w_sb, ws_sb = mx_tile("w_sb", S, U32), mx_tile("ws_sb", S, U8)
        wv_sb, wvs_sb = mx_tile("wv_sb", D, U32), mx_tile("wvs_sb", D, U8)
        xq = [mx_tile("xq%d" % b, S, U32) for b in range(B)]
        xs = [mx_tile("xs%d" % b, S, U8) for b in range(B)]
        vq = [mx_tile("vq%d" % b, D, U32) for b in range(B)]
        vs = [mx_tile("vs%d" % b, D, U8) for b in range(B)]
        pq, ps = mx_tile("pq", N_TILES * P, U32), mx_tile("ps", N_TILES * P, U8)
        oq = [mx_tile("oq%d" % b, S, U32) for b in range(B)]
        os_ = mx_tile("os_", B * S, U8)
        vn = [keep.tile([P, PACK, D], BF16, name="vn%d" % b, align_bytes=MX_ALIGN) for b in range(B)]
        og = [keep.tile([P, S, PACK], BF16, name="og%d" % b, align_bytes=MX_ALIGN) for b in range(B)]
        rm = keep.tile([P, TILES, S], F32, name="rm")
        lg = keep.tile([P, N_TILES, S], F32, name="lg")
        nmax = keep.tile([P, N_TILES], F32, name="nmax")
        tot = keep.tile([P, N_TILES], F32, name="tot")
        rinv = keep.tile([P, N_TILES], F32, name="rinv")
        mix_bf = keep.tile([P, 2], BF16, name="mix_bf")
        mix_f = keep.tile([P, 2], F32, name="mix_f")
        u_bf = keep.tile([P, TILES], BF16, name="u_bf")
        u_f = keep.tile([P, TILES], F32, name="u_f")
        c_row = keep.tile([P, S], BF16, name="c_row")
        ones = keep.tile([P, P], BF16, name="ones")
        ident = keep.tile([P, P], F32, name="ident")
        c_ps = psum.tile([P, S], F32, name="c_ps")

        held = {}

        def bank():
            acc = psum.tile([P, D], F32, name="acc", bufs=ROTATING_BANKS)
            return acc

        def stage(name):
            tl = keep.tile([P, D * PACK], BF16, name=name, align_bytes=MX_ALIGN)
            return tl

        def cols(n, cnt=1):
            return slice(P * n, P * (n + cnt))

        def tile_of(loads, tiles, n):
            return [tl[:, n - n0, :] for (n0, n1), tl in zip(loads, tiles) if n0 <= n < n1][0]

        def mx_matmul(out, lq, ls, rq, rs):
            nc.tensor.matmul_mx(
                out=out, lhsT=lq.bitcast(X4), lhsT_scale=ls, rhs=rq.bitcast(X4), rhs_scale=rs, start=True, stop=True
            )

        def quantise(words, scales, src):
            nc.vector.quantize_mx(out=words.bitcast(X4), scales=scales, in_=src)

        def turn(dst, src):
            words = src.bitcast(F32)
            for h in range(PAIR):
                nc.tensor.transpose(dst[:, h, :], words[:, h : PAIR * P : PAIR], ident[:])

        def turned(acc):
            return acc[:].rearrange("p (i h n) -> p i h n", i=PAIR, h=PAIR)

        def load_rows(dst, rows, t0, t1):
            nc.sync.dma_start(out=dst[:], in_=rows.rearrange("(p t) f -> p t f", t=TILES)[:, t0:t1, :])

        def load_x(g):
            b, t0 = divmod(X_LOADS[g][0], TILES)
            load_rows(x_sb[g], x[b], t0, X_LOADS[g][1] - TILES * b)

        def load_rnd(g):
            load_rows(rnd_sb[g], rnd, *RND_LOADS[g])

        def load_words(dst, src):
            nc.sync.dma_start(out=dst[:].bitcast(I32), in_=src[0].rearrange("p n t -> p (n t)").bitcast(I32))

        def load_scales(dst, src):
            for r in range(SCALE_ROWS):
                nc.sync.dma_start(out=dst[r:P:QUADRANT, :].bitcast(I32), in_=src[0, r::SCALE_ROWS, :].bitcast(I32))

        def x_turn(n, cnt):
            held["xt", n] = turned(bank())
            for i in range(cnt):
                turn(held["xt", n][:, i], tile_of(X_LOADS, x_sb, n + i))

        def x_copy(n, cnt):
            held["xg", n] = stage("stage_x%d" % n)[:, 0 : cnt * P * PACK]
            nc.scalar.copy(
                out=held["xg", n].bitcast(F32).rearrange("p (i n h) -> p i n h", i=cnt, h=PAIR),
                in_=held["xt", n][:, 0:cnt].rearrange("p i h n -> p i n h"),
            )

        def x_quant(n, cnt):
            b, t = divmod(n, TILES)
            quantise(xq[b][:, cols(t, cnt)], xs[b][:, cols(t, cnt)], held["xg", n])

        def rnd_mix_scalar(t):
            nc.scalar.activation(out=rm[:, t, :], in_=tile_of(RND_LOADS, rnd_sb, t), func=ACT.Copy, scale=mix_f[:, 1:2])

        def rnd_mix_gpsimd(t):
            nc.gpsimd.tensor_scalar(
                out=rm[:, t, :], in0=tile_of(RND_LOADS, rnd_sb, t), scalar1=mix_bf[:, 1:2], scalar2=0.0,
                op0=ALU.mult, op1=ALU.add,
            )

        def syn(n):
            b, t = divmod(n, TILES)
            held["syn", n] = bank()
            mx_matmul(held["syn", n][:], xq[b][:, cols(t)], xs[b][:, cols(t)], w_sb[:], ws_sb[:])

        def logit(n):
            nc.vector.scalar_tensor_tensor(
                out=lg[:, n, :], in0=held["syn", n][:], scalar=mix_bf[:, 0:1], in1=rm[:, n % TILES, :],
                op0=ALU.mult, op1=ALU.add,
            )

        def row_max(n):
            nc.vector.tensor_reduce(out=nmax[:, n : n + 1], in_=lg[:, n, :], axis=AXIS.X, op=ALU.max, negate=True)

        def expo(n):
            e = work.tile([P, S], F32, name="e")
            nc.scalar.activation(
                out=e[:], in_=lg[:, n, :], func=ACT.Exp, bias=nmax[:, n : n + 1], scale=1.0,
                accum_out=tot[:, n : n + 1],
            )
            held["e", n] = e

        def recip(a):
            nc.vector.reciprocal(rinv[:, a : a + PAIR], tot[:, a : a + PAIR])

        def scale_and_turn(n):
            scale(n)
            p_turn(n)

        def scale(n):
            pc = work.tile([P, S], BF16, name="pc", align_bytes=MX_ALIGN)
            nc.vector.scalar_tensor_tensor(
                out=pc[:], in0=held["e", n][:], scalar=rinv[:, n : n + 1], in1=c_ps[:], op0=ALU.mult, op1=ALU.mult
            )
            held["pc", n] = pc

        def p_turn(n):
            if n % PAIR == 0:
                held["pt", n] = turned(bank())
            turn(held["pt", n - n % PAIR][:, n % PAIR], held["pc", n][:])

        def p_copy(a):
            held["pg", a] = stage("stage_p%d" % a)[:, 0 : PAIR * P * PACK]
            nc.scalar.copy(
                out=held["pg", a].bitcast(F32).rearrange("p (n i h) -> p n i h", i=PAIR, h=PAIR),
                in_=held["pt", a].rearrange("p i h n -> p n i h"),
            )

        def p_copy_unit(n):
            a, half = n - n % PAIR, slice(P // PAIR * (n % PAIR), P // PAIR * (n % PAIR + 1))
            held["pg1", n] = stage("stage_u%d" % n)[:, 0 : P * PACK]
            nc.scalar.copy(
                out=held["pg1", n].bitcast(F32).rearrange("p (n i h) -> p n i h", i=PAIR, h=PAIR),
                in_=held["pt", a].rearrange("p i h n -> p n i h")[:, half],
            )

        def p_quant_unit(n):
            quantise(pq[:, cols(n)], ps[:, cols(n)], held["pg1", n])

        def p_quant(a):
            quantise(pq[:, cols(a, PAIR)], ps[:, cols(a, PAIR)], held["pg", a])

        def v_mm(n):
            b, t = divmod(n, TILES)
            held["v", n] = bank()
            mx_matmul(held["v", n][:], xq[b][:, cols(t)], xs[b][:, cols(t)], wv_sb[:], wvs_sb[:])

        def v_gain(n):
            b, t = divmod(n, TILES)
            nc.scalar.activation(
                out=vn[b][:, t, :].rearrange("p (j m) -> p j m", j=PACK),
                in_=held["v", n][:].rearrange("p (m j) -> p j m", j=PACK),
                func=ACT.Copy, scale=u_f[:, t : t + 1],
            )

        def v_pack(b, after):
            held["vg", b] = stage(after)[:]
            nc.gpsimd.tensor_scalar(
                out=held["vg", b].rearrange("p (c t) -> p c t", t=PACK), in0=vn[b][:].rearrange("p t c -> p c t"),
                scalar1=1.0, scalar2=0.0, op0=ALU.mult, op1=ALU.add,
            )

        def v_quant(b):
            quantise(vq[b][:], vs[b][:], held["vg", b])

        def unit_tokens(n):
            half, t0 = n % PAIR, n % TILES - n % PAIR
            return slice(P // PAIR * half, P // PAIR * (half + 1)), slice(t0, t0 + PAIR)

        def rows_mm(n):
            b = n // TILES
            held["rows", n] = bank()
            mx_matmul(held["rows", n][:], pq[:, cols(n)], ps[:, cols(n)], vq[b][:], vs[b][:])

        def planes_mm(n):
            b = n // TILES
            held["planes", n] = bank()
            for j in range(PACK):
                mx_matmul(held["planes", n][:, cols(j)], vq[b][:, cols(j)], vs[b][:, cols(j)], pq[:, cols(n)], ps[:, cols(n)])

        def rows_out(n, queue, copy=nc.scalar.copy):
            ob = work.tile([P, D], F32, name="ob")
            copy(
                out=ob[:].rearrange("p (m j) -> p m j", j=PACK),
                in_=held["rows", n][:].rearrange("p (j m) -> p m j", j=PACK),
            )
            held["ob", n] = ob
            parts, tiles = unit_tokens(n)
            queue.dma_start(out=out_0[n // TILES].rearrange("(p t) d -> p t d", t=TILES)[parts, tiles, :], in_=ob[:])

        def planes_copy(n, copy):
            parts, tiles = unit_tokens(n)
            copy(
                out=og[n // TILES][:].rearrange("m (p t) j -> m p t j", t=TILES)[:, parts, tiles, :],
                in_=held["planes", n][:].rearrange("m (j p i) -> m p i j", j=PACK, i=PAIR),
            )

        def rows_round(n, buffer):
            held["oc", n] = stage(buffer)[:, 0:D]
            nc.gpsimd.tensor_scalar(
                out=held["oc", n], in0=held["ob", n][:], scalar1=1.0, scalar2=0.0, op0=ALU.mult, op1=ALU.add
            )

        def rows_turned_unit(n, copy):
            parts, tiles = unit_tokens(n)
            words = og[n // TILES][:].rearrange("m s j -> m (s j)").bitcast(F32)
            copy(
                out=words.rearrange("m (p t h) -> m p t h", t=TILES, h=PAIR)[:, parts, tiles, :],
                in_=held["ot1", n].rearrange("m h (p i) -> m p i h", i=PAIR),
            )

        def rows_turn_unit(n):
            held["ot1", n] = turned(bank())[:, 0]
            turn(held["ot1", n], held["oc", n])

        def planes_quant(b, half):
            here = slice(HALF * half, HALF * (half + 1))
            there = slice(S * b + here.start, S * b + here.stop)
            quantise(oq[b][:, here], os_[:, there], og[b][:, here, :].rearrange("m s j -> m (s j)"))

        def planes_out(b, half):
            planes_quant(b, half)
            codes_out(b, slice(HALF * half, HALF * (half + 1)))

        def codes_out(b, here):
            there = slice(S * b + here.start, S * b + here.stop)
            nc.sync.dma_start(
                out=out_1[0][:, there, :].rearrange("m s j -> m (s j)").bitcast(I32), in_=oq[b][:, here].bitcast(I32)
            )

        def scales_out(there, queue):
            for r in range(SCALE_ROWS):
                queue.dma_start(
                    out=out_2[0, r::SCALE_ROWS, there].bitcast(I32), in_=os_[r:P:QUADRANT, there].bitcast(I32)
                )

        def warm_up(after):
            unread = bank()
            nc.tensor.matmul(unread[:, 0:WARM_WIDTH], lhsT=ident[:], rhs=after[:, 0:WARM_WIDTH], start=True, stop=True)

        def head_warm_up(count):
            unread = bank()
            for _ in range(count):
                nc.tensor.matmul(unread[:], lhsT=c_row[:, 0:P], rhs=c_row[:], start=True, stop=True)

        on_scalar, on_vector = nc.scalar.copy, nc.vector.tensor_copy

        nc.vector.memset(c_row[:], 0.0)
        nc.vector.memset(ws_sb[:].bitcast(I32), 0)
        nc.vector.memset(wvs_sb[:].bitcast(I32), 0)
        nc.gpsimd.dma_start(out=mix_bf[:], in_=mix.partition_broadcast(P))
        make_identity(nc, ident[:])
        nc.scalar.activation(out=ones[:], in_=c_row[:, 0:P], func=ACT.Copy, bias=1.0)
        for g in range(3):
            load_x(g)
        load_scales(ws_sb, w_scales)
        load_words(w_sb, w_words)
        nc.gpsimd.dma_start(out=u_bf[:], in_=u.rearrange("(p t) -> p t", t=TILES))
        load_rnd(0)
        load_rnd(1)
        load_words(wv_sb, wv_words)
        load_scales(wvs_sb, wv_scales)
        load_rnd(2)

        head_warm_up(2)
        nc.sync.dma_start(out=c_row[0:1, :], in_=c.rearrange("(o k) -> o k", o=1))
        load_x(3)
        x_turn(0, 1)
        x_turn(1, 1)
        x_turn(2, PAIR)
        x_copy(0, 1)
        x_copy(1, 1)
        nc.scalar.copy(out=mix_f[:], in_=mix_bf[:])
        x_copy(2, PAIR)
        rnd_mix_scalar(0)
        rnd_mix_scalar(1)
        nc.scalar.copy(out=u_f[:], in_=u_bf[:])
        for n in range(PAIR):
            x_quant(n, 1)
            syn(n)
        for n in range(PAIR):
            rnd_mix_gpsimd(PAIR + n)
            v_mm(n)
        x_quant(2, PAIR)
        logit(0)
        syn(2)
        v_mm(2)
        logit(1)
        v_gain(0)
        v_mm(3)
        syn(3)
        nc.tensor.matmul(c_ps[:], lhsT=ones[:], rhs=c_row[:], start=True, stop=True)
        row_max(0)
        row_max(1)
        v_gain(1)
        expo(0)
        expo(1)
        x_turn(4, PAIR)
        x_turn(6, PAIR)
        logit(2)
        logit(3)
        row_max(2)
        recip(0)
        row_max(3)
        x_copy(4, PAIR)
        x_copy(6, PAIR)
        v_gain(2)
        v_gain(3)
        x_quant(4, PAIR)
        warm_up(lg[:, 3, :])
        syn(4)
        v_mm(4)
        syn(5)
        x_quant(6, PAIR)
        v_pack(0, "stage_x6")
        v_mm(5)
        scale_and_turn(0)
        scale_and_turn(1)
        v_mm(6)
        v_mm(7)
        expo(2)
        expo(3)
        v_gain(4)
        p_copy(0)
        v_gain(5)

        logit(4)
        logit(5)
        row_max(4)
        recip(2)
        row_max(5)
        syn(6)
        syn(7)
        warm_up(lg[:, 5, :])
        p_quant(0)
        v_quant(0)
        v_gain(6)
        v_gain(7)
        v_pack(1, "stage_p0")
        rows_mm(0)
        rows_mm(1)
        scale_and_turn(2)
        scale_and_turn(3)
        planes_mm(0)
        expo(4)
        expo(5)
        rows_out(0, nc.sync)
        rows_out(1, nc.sync)
        p_copy(2)

        logit(6)
        warm_up(lg[:, 6, :])
        logit(7)
        row_max(6)
        recip(4)
        row_max(7)
        p_quant(2)
        rows_round(1, "stage_p2")
        rows_mm(2)
        planes_mm(2)
        rows_mm(3)
        scale_and_turn(4)
        scale_and_turn(5)
        expo(6)
        expo(7)
        planes_copy(0, on_scalar)
        rows_turn_unit(1)
        planes_mm(3)
        warm_up(lg[:, 7, :])
        recip(6)
        v_quant(1)
        rows_out(2, nc.sync)
        planes_copy(2, on_scalar)
        p_copy(4)
        rows_turned_unit(1, on_scalar)
        rows_out(3, nc.sync)

        scale_and_turn(6)
        scale_and_turn(7)
        p_quant(4)
        rows_mm(4)
        planes_mm(4)
        rows_mm(5)
        planes_copy(3, on_vector)
        planes_mm(5)
        p_copy_unit(6)
        p_copy_unit(7)
        planes_out(0, 0)
        p_quant_unit(6)
        planes_out(0, 1)
        p_quant_unit(7)
        rows_out(4, nc.sync)
        planes_mm(6)
        rows_mm(6)
        planes_mm(7)
        rows_mm(7)
        rows_out(5, nc.sync)
        planes_copy(4, on_vector)
        planes_copy(6, on_vector)
        planes_copy(5, on_vector)
        rows_out(6, nc.sync)
        planes_copy(7, on_scalar)
        planes_out(1, 0)
        planes_out(1, 1)
        scales_out(slice(0, B * S), nc.sync)
        rows_out(7, nc.scalar)
